import numpy as np
import ml_dtypes


def mxq(x, axis, fmt="e4m3"):
    dtype, down = {"e4m3": (ml_dtypes.float8_e4m3fn, 7), "e5m2": (ml_dtypes.float8_e5m2, 14)}[fmt]
    v = np.moveaxis(np.asarray(x, np.float32).astype(ml_dtypes.bfloat16).astype(np.float64), axis, -1)
    blocks = v.reshape(v.shape[:-1] + (-1, 32))
    amax = np.abs(blocks).max(-1, keepdims=True)
    byte = np.maximum(np.where(amax > 0, np.frexp(amax)[1] - 1 + 127, 0) - down, 1)
    scale = np.exp2(byte - 127.0)
    codes = (blocks / scale).astype(np.float32).astype(dtype).astype(np.float64)
    return np.moveaxis((codes * scale).reshape(v.shape), -1, axis)


WIDE = False


def mx_kscale(k):
    if not WIDE:
        return np.ones(k)
    levels = np.array([10, -10, 5, -5, 0])
    if k % 512:
        return np.exp2(np.random.permutation(np.resize(levels, k // 32))).repeat(32)
    a = np.empty((k // 512, 16))
    for p in range(k // 512):
        a[p, :8] = np.random.permutation(np.resize(levels, 8))
        for g in range(8):
            far = levels[np.abs(levels - a[p, g]) >= 10]
            a[p, g + 8] = far[np.random.randint(len(far))]
    return np.exp2(a.ravel()).repeat(32)


def f64(x):
    return np.asarray(x).astype(np.float64)


def striped(idx):
    return np.tile(idx.reshape(-1, 16).T, (8, 1)).astype(np.uint16)


def unstriped(offs):
    return offs[:16].T.reshape(-1).astype(np.int64)


K, T, D, S, V, N = 1024, 1024, 8, 4096, 512, 256


def setup_inputs():
    n = np.random.standard_normal
    s = mx_kscale(K)[:, None]
    return {
        "xT": (n((K, T)) * s).astype(np.float32),
        "w": (n((K, N)) / np.sqrt(K) / s).astype(np.float32),
        "offs": striped(np.concatenate([np.random.permutation(T)[:V] for _ in range(D)])),
    }


def reference(xT, w, offs):
    idx = unstriped(offs)
    x = np.empty((K, V))
    for l in range(D):
        r = l // 4 * (4 * K // D) + l % 4 + 4 * np.arange(K // D)
        x[r] = f64(xT)[r][:, idx[l * V:(l + 1) * V]]
    xq = mxq(x, 0, "e4m3")
    return mxq(f64(w), 0, "e4m3").T @ xq

@@ -1,0 +1,195 @@
+from contextlib import ExitStack
+
+import concourse.mybir as mybir
+
+K, T, D, V, N = 1024, 1024, 8, 512, 256
+FLOPS = 2 * K * N * V
+
+F32 = mybir.dt.float32
+BF16 = mybir.dt.bfloat16
+U32 = mybir.dt.uint32
+U16 = mybir.dt.uint16
+U8 = mybir.dt.uint8
+FP8X4 = mybir.dt.float8_e4m3fn_x4
+
+COPY = mybir.ActivationFunctionType.Copy
+
+P = 128
+PACK = 4
+K_PASS = P * PACK
+PASSES = K // K_PASS
+HALF = V // 2
+
+
+def tile_picked_grid_lin_none_sub_l_kernel(tc, xT, w, offs, out):
+    nc = tc.nc
+    with ExitStack() as ctx:
+        keep = ctx.enter_context(tc.tile_pool(name="keep", bufs=1))
+        psum = ctx.enter_context(tc.psum_pool(name="psum", bufs=1))
+
+        offsets = keep.tile([P, D * V // 16], U16, name="offsets")
+
+        warm = keep.tile([P, 1], F32, name="warm")
+        warm_out = keep.tile([P, 1], F32, name="warm_out")
+        nc.vector.memset(warm[:], 0.0)
+        nc.scalar.activation(warm_out[:], warm[:], COPY)
+
+        tables = {}
+        w_raw = {}
+
+        def load_level(l):
+            g, j = divmod(l, PACK)
+            table = keep.tile([P, T], F32, name=f"table{l}", tag="table4" if l == 4 else f"table{l}", align_bytes=64)
+            rows = xT[g * K_PASS : (g + 1) * K_PASS, :].rearrange("(p j) t -> p j t", j=PACK)
+            nc.sync.dma_start(out=table[:], in_=rows[:, j, :])
+            tables[l] = table
+
+        def load_w(g):
+            raw = keep.tile([P, PACK, N], F32, name=f"w_raw{g}", align_bytes=64)
+            nc.sync.dma_start(out=raw[:], in_=w[g * K_PASS : (g + 1) * K_PASS, :].rearrange("(p j) n -> p j n", j=PACK))
+            w_raw[g] = raw
+
+        load_level(0)
+        nc.sync.dma_start(offsets[:], offs)
+        load_level(2)
+        load_level(1)
+        load_level(3)
+        load_level(4)
+        load_level(6)
+        load_w(0)
+        load_level(5)
+        load_level(7)
+        load_w(1)
+
+        picked = [keep.tile([P, PACK, V], F32, name=f"picked{g}", align_bytes=64) for g in range(PASSES)]
+        grouped = [keep.tile([P, V, PACK], BF16, name=f"grouped{g}", align_bytes=64) for g in range(PASSES)]
+        codes = [None, keep.tile([P, V], U32, name="codes1", align_bytes=64)]
+        scales = [keep.tile([P, V], U8, name=f"scales{g}", align_bytes=64) for g in range(PASSES)]
+        w_grouped = [keep.tile([P, N, PACK], BF16, name=f"w_grouped{g}", align_bytes=64) for g in range(PASSES)]
+        w_codes = [keep.tile([P, N], U32, name=f"w_codes{g}", align_bytes=64) for g in range(PASSES)]
+        w_scales = [keep.tile([P, N], U8, name=f"w_scales{g}", align_bytes=64) for g in range(PASSES)]
+        acc = [[psum.tile([P, HALF], F32, name=f"acc{m}{c}") for c in range(2)] for m in range(2)]
+        res = [[keep.tile([P, HALF], F32, name=f"res{m}{c}", align_bytes=64) for c in range(2)] for m in range(2)]
+
+        def gather(l, v0, v1):
+            g, j = divmod(l, PACK)
+            c0 = l * V // 16
+            nc.vector.tensor_copy(
+                picked[g][:, j, v0:v1],
+                tables[l][:].indirect(offsets[:, c0 + v0 // 16 : c0 + v1 // 16]),
+            )
+
+        def interleave(copy, g, j0, j1, v0, v1):
+            copy(
+                out=grouped[g][:, v0:v1, j0:j1],
+                in_=picked[g][:, j0:j1, v0:v1].rearrange("p j v -> p v j"),
+            )
+
+        def quantize(g, v0, v1):
+            nc.vector.quantize_mx(
+                out=codes[g][:, v0:v1].bitcast(FP8X4),
+                scales=scales[g][:, v0:v1],
+                in_=grouped[g][:, v0:v1, :].rearrange("p v j -> p (v j)"),
+            )
+
+        def interleave_all(copy, dst, src):
+            copy(
+                out=dst.rearrange("p (c i) j -> p c j i", i=4),
+                in_=src.rearrange("p j (c i) -> p c j i", i=4),
+            )
+
+        def interleave_w(copy, g, n0, n1):
+            interleave_all(copy, w_grouped[g][:, n0:n1, :], w_raw[g][:, :, n0:n1])
+
+        def quantize_w(g, n0, n1):
+            nc.vector.quantize_mx(
+                out=w_codes[g][:, n0:n1].bitcast(FP8X4),
+                scales=w_scales[g][:, n0:n1],
+                in_=w_grouped[g][:, n0:n1, :].rearrange("p n j -> p (n j)"),
+            )
+
+        def multiply(g, m, c):
+            mc = slice(m * P, (m + 1) * P)
+            vc = slice(c * HALF, (c + 1) * HALF)
+            nc.tensor.matmul_mx(
+                out=acc[m][c][:],
+                lhsT=w_codes[g][:, mc].bitcast(FP8X4),
+                lhsT_scale=w_scales[g][:, mc],
+                rhs=codes[g][:, vc].bitcast(FP8X4),
+                rhs_scale=scales[g][:, vc],
+                start=(g == 0),
+                stop=(g == PASSES - 1),
+            )
+
+        def store(copy, m, c):
+            copy(out=res[m][c][:], in_=acc[m][c][:])
+            nc.sync.dma_start(out=out[m * P : (m + 1) * P, c * HALF : (c + 1) * HALF], in_=res[m][c][:])
+
+        sc, vc = nc.scalar.copy, nc.vector.tensor_copy
+
+        narrow = {}
+
+        def cast(engine_copy, l):
+            narrow[l] = keep.tile([P, T], BF16, name=f"narrow{l}", align_bytes=64)
+            engine_copy(out=narrow[l][:], in_=tables[l][:])
+
+        def scalar_gather(l, v0, v1):
+            g, j = divmod(l, PACK)
+            c0 = l * V // 16
+            nc.scalar.activation(
+                grouped[g][:, v0:v1, j],
+                narrow[l][:].indirect(offsets[:, c0 + v0 // 16 : c0 + v1 // 16]),
+                COPY,
+            )
+
+        def vector_gather(l, v0, v1):
+            g, j = divmod(l, PACK)
+            c0 = l * V // 16
+            nc.vector.tensor_copy(
+                grouped[g][:, v0:v1, j],
+                tables[l][:].indirect(offsets[:, c0 + v0 // 16 : c0 + v1 // 16]),
+            )
+
+        cast(vc, 0)
+        scalar_gather(0, 0, V)
+        vector_gather(2, 0, V)
+        cast(vc, 1)
+        scalar_gather(1, 0, V)
+        vector_gather(3, 0, V)
+        cast(vc, 4)
+        scalar_gather(4, 0, V)
+        codes[0] = keep.tile([P, V], U32, name="codes0", tag="table4", align_bytes=64)
+        quantize(0, 0, V)
+        vector_gather(6, 0, V)
+        interleave_w(sc, 0, 0, N)
+        cast(vc, 5)
+        scalar_gather(5, 0, V)
+        quantize_w(0, 0, N)
+        for m in range(2):
+            for c in range(2):
+                multiply(0, m, c)
+        spin = psum.tile([P, V], F32, name="spin")
+        nc.tensor.matmul_mx(
+            out=spin[:],
+            lhsT=w_codes[0][:, 0:P].bitcast(FP8X4),
+            lhsT_scale=w_scales[0][:, 0:P],
+            rhs=codes[0][:].bitcast(FP8X4),
+            rhs_scale=scales[0][:],
+            start=True,
+            stop=True,
+        )
+        vector_gather(7, 0, HALF)
+        interleave_w(sc, 1, 0, P)
+        interleave_w(sc, 1, P, N)
+        vector_gather(7, HALF, V)
+        quantize(1, 0, HALF)
+        quantize_w(1, 0, P)
+        quantize(1, HALF, V)
+        quantize_w(1, P, N)
+        for m in range(2):
+            for c in range(2):
+                multiply(1, m, c)
+        store(sc, 0, 0)
+        store(vc, 0, 1)
+        store(sc, 1, 0)
+        store(vc, 1, 1)

@@ -7,6 +7,7 @@ FLOPS = 2 * K * N * V
 
 F32 = mybir.dt.float32
 BF16 = mybir.dt.bfloat16
+I32 = mybir.dt.int32
 U32 = mybir.dt.uint32
 U16 = mybir.dt.uint16
 U8 = mybir.dt.uint8
@@ -34,89 +35,112 @@ def tile_picked_grid_lin_none_sub_l_kernel(tc, xT, w, offs, out):
         nc.vector.memset(warm[:], 0.0)
         nc.scalar.activation(warm_out[:], warm[:], COPY)
 
+        sc, vc = nc.scalar.copy, nc.vector.tensor_copy
         tables = {}
         w_raw = {}
+        narrow = {}
 
-        def load_level(l):
+        def load_levels(l, count):
             g, j = divmod(l, PACK)
-            table = keep.tile([P, T], F32, name=f"table{l}", tag="table4" if l == 4 else f"table{l}", align_bytes=64)
+            table = keep.tile([P, count, T], F32, name=f"table{l}", align_bytes=64)
             rows = xT[g * K_PASS : (g + 1) * K_PASS, :].rearrange("(p j) t -> p j t", j=PACK)
-            nc.sync.dma_start(out=table[:], in_=rows[:, j, :])
-            tables[l] = table
+            nc.sync.dma_start(out=table[:], in_=rows[:, j : j + count, :])
+            for i in range(count):
+                tables[l + i] = table[:, i, :]
 
-        def load_w(g):
-            raw = keep.tile([P, PACK, N], F32, name=f"w_raw{g}", align_bytes=64)
-            nc.sync.dma_start(out=raw[:], in_=w[g * K_PASS : (g + 1) * K_PASS, :].rearrange("(p j) n -> p j n", j=PACK))
-            w_raw[g] = raw
+        def load_w(g, m0, m1):
+            raw = keep.tile([P, PACK, (m1 - m0) * P], F32, name=f"w_raw{g}{m0}", align_bytes=64)
+            rows = w[g * K_PASS : (g + 1) * K_PASS, m0 * P : m1 * P].rearrange("(p j) n -> p j n", j=PACK)
+            nc.sync.dma_start(out=raw[:], in_=rows)
+            for m in range(m0, m1):
+                w_raw[g, m] = raw[:, :, (m - m0) * P : (m - m0 + 1) * P]
 
-        load_level(0)
+        def listed(l, v0, v1):
+            c0 = l * V // 16
+            return offsets[:, c0 + v0 // 16 : c0 + v1 // 16]
+
+        def cast(copy, l):
+            narrow[l] = keep.tile([P, T], BF16, name=f"narrow{l}", align_bytes=64)
+            copy(out=narrow[l][:], in_=tables[l])
+
+        load_levels(0, 1)
         nc.sync.dma_start(offsets[:], offs)
-        load_level(2)
-        load_level(1)
-        load_level(3)
-        load_level(4)
-        load_level(6)
-        load_w(0)
-        load_level(5)
-        load_level(7)
-        load_w(1)
+        load_levels(1, 1)
+        load_levels(2, 1)
+        load_levels(3, 1)
+        load_levels(4, 1)
+        load_levels(6, 1)
+        load_levels(5, 1)
+        load_levels(7, 1)
+        load_w(0, 0, 1)
+        load_w(0, 1, 2)
+        load_w(1, 0, 1)
+        load_w(1, 1, 2)
 
-        picked = [keep.tile([P, PACK, V], F32, name=f"picked{g}", align_bytes=64) for g in range(PASSES)]
-        grouped = [keep.tile([P, V, PACK], BF16, name=f"grouped{g}", align_bytes=64) for g in range(PASSES)]
-        codes = [None, keep.tile([P, V], U32, name="codes1", align_bytes=64)]
-        scales = [keep.tile([P, V], U8, name=f"scales{g}", align_bytes=64) for g in range(PASSES)]
-        w_grouped = [keep.tile([P, N, PACK], BF16, name=f"w_grouped{g}", align_bytes=64) for g in range(PASSES)]
-        w_codes = [keep.tile([P, N], U32, name=f"w_codes{g}", align_bytes=64) for g in range(PASSES)]
-        w_scales = [keep.tile([P, N], U8, name=f"w_scales{g}", align_bytes=64) for g in range(PASSES)]
+        pairs = {}
+        grouped = {}
+        grouped[0, 0] = keep.tile([P, V * PACK], BF16, name="grouped0", align_bytes=64)
+        for v0 in (0, HALF):
+            pairs[1, v0] = keep.tile([P, 2, HALF, 2], BF16, name=f"pairs1_{v0}", align_bytes=64)
+        codes = {}
+        scales = {}
+        w_grouped = {}
+        w_codes = {}
+        w_scales = {}
+        for g in range(PASSES):
+            for m in range(2):
+                w_grouped[g, m] = keep.tile([P, P, PACK], BF16, name=f"w_grouped{g}{m}", align_bytes=64)
+                w_codes[g, m] = keep.tile([P, P], U32, name=f"w_codes{g}{m}", align_bytes=64)
+                w_scales[g, m] = keep.tile([P, P], U8, name=f"w_scales{g}{m}", align_bytes=64)
         acc = [[psum.tile([P, HALF], F32, name=f"acc{m}{c}") for c in range(2)] for m in range(2)]
         res = [[keep.tile([P, HALF], F32, name=f"res{m}{c}", align_bytes=64) for c in range(2)] for m in range(2)]
 
         def gather(l, v0, v1):
             g, j = divmod(l, PACK)
-            c0 = l * V // 16
-            nc.vector.tensor_copy(
-                picked[g][:, j, v0:v1],
-                tables[l][:].indirect(offsets[:, c0 + v0 // 16 : c0 + v1 // 16]),
-            )
+            if (g, v0) in pairs:
+                dst = pairs[g, v0][:, j % 2, :, j // 2]
+            else:
+                dst = grouped[g, 0][:].rearrange("p (v t) -> p v t", t=PACK)[:, v0:v1, 2 * (j % 2) + j // 2]
+            if j % 2 == 0:
+                nc.scalar.activation(dst, narrow[l][:].indirect(listed(l, v0, v1)), COPY)
+            else:
+                nc.vector.tensor_copy(dst, tables[l].indirect(listed(l, v0, v1)))
 
-        def interleave(copy, g, j0, j1, v0, v1):
+        def weave(copy, word, g, v0, v1, tag):
+            grouped[g, v0] = keep.tile([P, (v1 - v0) * PACK], BF16, name=f"grouped{g}_{v0}", tag=tag, align_bytes=64)
             copy(
-                out=grouped[g][:, v0:v1, j0:j1],
-                in_=picked[g][:, j0:j1, v0:v1].rearrange("p j v -> p v j"),
+                out=grouped[g, v0][:].bitcast(word).rearrange("p (v a) -> p v a", a=2),
+                in_=pairs[g, v0][:].rearrange("p a v e -> p a (v e)").bitcast(word).rearrange("p a v -> p v a"),
             )
 
-        def quantize(g, v0, v1):
-            nc.vector.quantize_mx(
-                out=codes[g][:, v0:v1].bitcast(FP8X4),
-                scales=scales[g][:, v0:v1],
-                in_=grouped[g][:, v0:v1, :].rearrange("p v j -> p (v j)"),
-            )
+        def quantize(g, v0, v1, tag):
+            words = keep.tile([P, v1 - v0], U32, name=f"codes{g}_{v0}", tag=tag, align_bytes=64)
+            plane = keep.tile([P, v1 - v0], U8, name=f"scales{g}_{v0}", align_bytes=64)
+            nc.vector.quantize_mx(out=words[:].bitcast(FP8X4), scales=plane[:], in_=grouped[g, v0][:])
+            for c0 in range(v0, v1, HALF):
+                codes[g, c0 // HALF] = words[:, c0 - v0 : c0 - v0 + HALF]
+                scales[g, c0 // HALF] = plane[:, c0 - v0 : c0 - v0 + HALF]
 
-        def interleave_all(copy, dst, src):
+        def interleave_w(copy, g, m):
             copy(
-                out=dst.rearrange("p (c i) j -> p c j i", i=4),
-                in_=src.rearrange("p j (c i) -> p c j i", i=4),
+                out=w_grouped[g, m][:].rearrange("p (c i) (e h) -> p c e h i", i=4, h=2),
+                in_=w_raw[g, m].rearrange("p (h e) (c i) -> p c e h i", i=4, h=2),
             )
 
-        def interleave_w(copy, g, n0, n1):
-            interleave_all(copy, w_grouped[g][:, n0:n1, :], w_raw[g][:, :, n0:n1])
-
-        def quantize_w(g, n0, n1):
+        def quantize_w(g, m):
             nc.vector.quantize_mx(
-                out=w_codes[g][:, n0:n1].bitcast(FP8X4),
-                scales=w_scales[g][:, n0:n1],
-                in_=w_grouped[g][:, n0:n1, :].rearrange("p n j -> p (n j)"),
+                out=w_codes[g, m][:].bitcast(FP8X4),
+                scales=w_scales[g, m][:],
+                in_=w_grouped[g, m][:].rearrange("p n j -> p (n j)"),
             )
 
         def multiply(g, m, c):
-            mc = slice(m * P, (m + 1) * P)
-            vc = slice(c * HALF, (c + 1) * HALF)
             nc.tensor.matmul_mx(
                 out=acc[m][c][:],
-                lhsT=w_codes[g][:, mc].bitcast(FP8X4),
-                lhsT_scale=w_scales[g][:, mc],
-                rhs=codes[g][:, vc].bitcast(FP8X4),
-                rhs_scale=scales[g][:, vc],
+                lhsT=w_codes[g, m][:].bitcast(FP8X4),
+                lhsT_scale=w_scales[g, m][:],
+                rhs=codes[g, c].bitcast(FP8X4),
+                rhs_scale=scales[g, c],
                 start=(g == 0),
                 stop=(g == PASSES - 1),
             )
@@ -125,70 +149,43 @@ def tile_picked_grid_lin_none_sub_l_kernel(tc, xT, w, offs, out):
             copy(out=res[m][c][:], in_=acc[m][c][:])
             nc.sync.dma_start(out=out[m * P : (m + 1) * P, c * HALF : (c + 1) * HALF], in_=res[m][c][:])
 
-        sc, vc = nc.scalar.copy, nc.vector.tensor_copy
-
-        narrow = {}
-
-        def cast(engine_copy, l):
-            narrow[l] = keep.tile([P, T], BF16, name=f"narrow{l}", align_bytes=64)
-            engine_copy(out=narrow[l][:], in_=tables[l][:])
-
-        def scalar_gather(l, v0, v1):
-            g, j = divmod(l, PACK)
-            c0 = l * V // 16
-            nc.scalar.activation(
-                grouped[g][:, v0:v1, j],
-                narrow[l][:].indirect(offsets[:, c0 + v0 // 16 : c0 + v1 // 16]),
-                COPY,
-            )
-
-        def vector_gather(l, v0, v1):
-            g, j = divmod(l, PACK)
-            c0 = l * V // 16
-            nc.vector.tensor_copy(
-                grouped[g][:, v0:v1, j],
-                tables[l][:].indirect(offsets[:, c0 + v0 // 16 : c0 + v1 // 16]),
-            )
-
         cast(vc, 0)
-        scalar_gather(0, 0, V)
-        vector_gather(2, 0, V)
-        cast(vc, 1)
-        scalar_gather(1, 0, V)
-        vector_gather(3, 0, V)
+        gather(0, 0, V)
+        gather(1, 0, V)
+        cast(vc, 2)
+        gather(2, 0, V)
+        gather(3, 0, V)
         cast(vc, 4)
-        scalar_gather(4, 0, V)
-        codes[0] = keep.tile([P, V], U32, name="codes0", tag="table4", align_bytes=64)
-        quantize(0, 0, V)
-        vector_gather(6, 0, V)
-        interleave_w(sc, 0, 0, N)
-        cast(vc, 5)
-        scalar_gather(5, 0, V)
-        quantize_w(0, 0, N)
-        for m in range(2):
-            for c in range(2):
-                multiply(0, m, c)
-        spin = psum.tile([P, V], F32, name="spin")
-        nc.tensor.matmul_mx(
-            out=spin[:],
-            lhsT=w_codes[0][:, 0:P].bitcast(FP8X4),
-            lhsT_scale=w_scales[0][:, 0:P],
-            rhs=codes[0][:].bitcast(FP8X4),
-            rhs_scale=scales[0][:],
-            start=True,
-            stop=True,
-        )
-        vector_gather(7, 0, HALF)
-        interleave_w(sc, 1, 0, P)
-        interleave_w(sc, 1, P, N)
-        vector_gather(7, HALF, V)
-        quantize(1, 0, HALF)
-        quantize_w(1, 0, P)
-        quantize(1, HALF, V)
-        quantize_w(1, P, N)
-        for m in range(2):
-            for c in range(2):
-                multiply(1, m, c)
+        gather(4, 0, HALF)
+        gather(4, HALF, V)
+        quantize(0, 0, V, "table4")
+        cast(vc, 6)
+        gather(6, 0, HALF)
+        gather(6, HALF, V)
+        gather(5, 0, HALF)
+        gather(5, HALF, V)
+        gather(7, 0, HALF)
+        gather(7, HALF, V)
+        interleave_w(sc, 0, 0)
+        weave(vc, I32, 1, 0, HALF, "grouped1a")
+        quantize_w(0, 0)
+        multiply(0, 0, 0)
+        multiply(0, 0, 1)
+        interleave_w(sc, 0, 1)
+        weave(vc, I32, 1, HALF, V, "w_grouped00")
+        quantize_w(0, 1)
+        multiply(0, 1, 0)
+        multiply(0, 1, 1)
+        quantize(1, 0, HALF, "w_raw01")
+        interleave_w(sc, 1, 0)
+        quantize_w(1, 0)
+        quantize(1, HALF, V, "w_raw10")
+        multiply(1, 0, 0)
+        multiply(1, 0, 1)
+        interleave_w(sc, 1, 1)
+        quantize_w(1, 1)
+        multiply(1, 1, 0)
+        multiply(1, 1, 1)
         store(sc, 0, 0)
         store(vc, 0, 1)
         store(sc, 1, 0)

@@ -77,11 +77,12 @@ def tile_picked_grid_lin_none_sub_l_kernel(tc, xT, w, offs, out):
         load_w(1, 0, 1)
         load_w(1, 1, 2)
 
+        spans = {0: [(0, V)], 1: [(0, HALF), (HALF, V)]}
         pairs = {}
         grouped = {}
-        grouped[0, 0] = keep.tile([P, V * PACK], BF16, name="grouped0", align_bytes=64)
-        for v0 in (0, HALF):
-            pairs[1, v0] = keep.tile([P, 2, HALF, 2], BF16, name=f"pairs1_{v0}", align_bytes=64)
+        for g in range(PASSES):
+            for v0, v1 in spans[g]:
+                pairs[g, v0] = keep.tile([P, 2, v1 - v0, 2], BF16, name=f"pairs{g}_{v0}", align_bytes=64)
         codes = {}
         scales = {}
         w_grouped = {}
@@ -97,10 +98,7 @@ def tile_picked_grid_lin_none_sub_l_kernel(tc, xT, w, offs, out):
 
         def gather(l, v0, v1):
             g, j = divmod(l, PACK)
-            if (g, v0) in pairs:
-                dst = pairs[g, v0][:, j % 2, :, j // 2]
-            else:
-                dst = grouped[g, 0][:].rearrange("p (v t) -> p v t", t=PACK)[:, v0:v1, 2 * (j % 2) + j // 2]
+            dst = pairs[g, v0][:, j % 2, :, j // 2]
             if j % 2 == 0:
                 nc.scalar.activation(dst, narrow[l][:].indirect(listed(l, v0, v1)), COPY)
             else:
@@ -145,9 +143,9 @@ def tile_picked_grid_lin_none_sub_l_kernel(tc, xT, w, offs, out):
                 stop=(g == PASSES - 1),
             )
 
-        def store(copy, m, c):
+        def store(copy, queue, m, c):
             copy(out=res[m][c][:], in_=acc[m][c][:])
-            nc.sync.dma_start(out=out[m * P : (m + 1) * P, c * HALF : (c + 1) * HALF], in_=res[m][c][:])
+            queue.dma_start(out=out[m * P : (m + 1) * P, c * HALF : (c + 1) * HALF], in_=res[m][c][:])
 
         cast(vc, 0)
         gather(0, 0, V)
@@ -155,28 +153,29 @@ def tile_picked_grid_lin_none_sub_l_kernel(tc, xT, w, offs, out):
         cast(vc, 2)
         gather(2, 0, V)
         gather(3, 0, V)
+        weave(sc, U32, 0, 0, V, "grouped0")
         cast(vc, 4)
         gather(4, 0, HALF)
         gather(4, HALF, V)
-        quantize(0, 0, V, "table4")
         cast(vc, 6)
         gather(6, 0, HALF)
         gather(6, HALF, V)
+        quantize(0, 0, V, "table6")
         gather(5, 0, HALF)
         gather(5, HALF, V)
         gather(7, 0, HALF)
         gather(7, HALF, V)
         interleave_w(sc, 0, 0)
-        weave(vc, I32, 1, 0, HALF, "grouped1a")
         quantize_w(0, 0)
         multiply(0, 0, 0)
         multiply(0, 0, 1)
+        weave(vc, I32, 1, 0, HALF, "w_raw00")
         interleave_w(sc, 0, 1)
-        weave(vc, I32, 1, HALF, V, "w_grouped00")
         quantize_w(0, 1)
         multiply(0, 1, 0)
         multiply(0, 1, 1)
-        quantize(1, 0, HALF, "w_raw01")
+        weave(vc, I32, 1, HALF, V, "w_raw01")
+        quantize(1, 0, HALF, "w_grouped01")
         interleave_w(sc, 1, 0)
         quantize_w(1, 0)
         quantize(1, HALF, V, "w_raw10")
@@ -186,7 +185,7 @@ def tile_picked_grid_lin_none_sub_l_kernel(tc, xT, w, offs, out):
         quantize_w(1, 1)
         multiply(1, 1, 0)
         multiply(1, 1, 1)
-        store(sc, 0, 0)
-        store(vc, 0, 1)
-        store(sc, 1, 0)
-        store(vc, 1, 1)
+        store(sc, nc.scalar, 0, 0)
+        store(vc, nc.sync, 0, 1)
+        store(sc, nc.scalar, 1, 0)
+        store(vc, nc.sync, 1, 1)

@@ -40,13 +40,12 @@ def tile_picked_grid_lin_none_sub_l_kernel(tc, xT, w, offs, out):
         w_raw = {}
         narrow = {}
 
-        def load_levels(l, count):
+        def load_level(l):
             g, j = divmod(l, PACK)
-            table = keep.tile([P, count, T], F32, name=f"table{l}", align_bytes=64)
+            table = keep.tile([P, T], F32, name=f"table{l}", align_bytes=64)
             rows = xT[g * K_PASS : (g + 1) * K_PASS, :].rearrange("(p j) t -> p j t", j=PACK)
-            nc.sync.dma_start(out=table[:], in_=rows[:, j : j + count, :])
-            for i in range(count):
-                tables[l + i] = table[:, i, :]
+            nc.sync.dma_start(out=table[:], in_=rows[:, j, :])
+            tables[l] = table[:]
 
         def load_w(g, m0, m1):
             raw = keep.tile([P, PACK, (m1 - m0) * P], F32, name=f"w_raw{g}{m0}", align_bytes=64)
@@ -63,15 +62,15 @@ def tile_picked_grid_lin_none_sub_l_kernel(tc, xT, w, offs, out):
             narrow[l] = keep.tile([P, T], BF16, name=f"narrow{l}", align_bytes=64)
             copy(out=narrow[l][:], in_=tables[l])
 
-        load_levels(0, 1)
+        load_level(0)
         nc.sync.dma_start(offsets[:], offs)
-        load_levels(1, 1)
-        load_levels(2, 1)
-        load_levels(3, 1)
-        load_levels(4, 1)
-        load_levels(6, 1)
-        load_levels(5, 1)
-        load_levels(7, 1)
+        load_level(2)
+        load_level(1)
+        load_level(3)
+        load_level(4)
+        load_level(5)
+        load_level(6)
+        load_level(7)
         load_w(0, 0, 1)
         load_w(0, 1, 2)
         load_w(1, 0, 1)
@@ -98,8 +97,8 @@ def tile_picked_grid_lin_none_sub_l_kernel(tc, xT, w, offs, out):
 
         def gather(l, v0, v1):
             g, j = divmod(l, PACK)
-            dst = pairs[g, v0][:, j % 2, :, j // 2]
-            if j % 2 == 0:
+            dst = pairs[g, v0][:, j // 2, :, j % 2]
+            if j < 2:
                 nc.scalar.activation(dst, narrow[l][:].indirect(listed(l, v0, v1)), COPY)
             else:
                 nc.vector.tensor_copy(dst, tables[l].indirect(listed(l, v0, v1)))
@@ -121,8 +120,8 @@ def tile_picked_grid_lin_none_sub_l_kernel(tc, xT, w, offs, out):
 
         def interleave_w(copy, g, m):
             copy(
-                out=w_grouped[g, m][:].rearrange("p (c i) (e h) -> p c e h i", i=4, h=2),
-                in_=w_raw[g, m].rearrange("p (h e) (c i) -> p c e h i", i=4, h=2),
+                out=w_grouped[g, m][:].rearrange("p (c i) j -> p c j i", i=4),
+                in_=w_raw[g, m].rearrange("p j (c i) -> p c j i", i=4),
             )
 
         def quantize_w(g, m):
@@ -149,20 +148,20 @@ def tile_picked_grid_lin_none_sub_l_kernel(tc, xT, w, offs, out):
 
         cast(vc, 0)
         gather(0, 0, V)
-        gather(1, 0, V)
-        cast(vc, 2)
         gather(2, 0, V)
+        cast(vc, 1)
+        gather(1, 0, V)
         gather(3, 0, V)
         weave(sc, U32, 0, 0, V, "grouped0")
         cast(vc, 4)
         gather(4, 0, HALF)
         gather(4, HALF, V)
-        cast(vc, 6)
-        gather(6, 0, HALF)
-        gather(6, HALF, V)
-        quantize(0, 0, V, "table6")
+        cast(vc, 5)
         gather(5, 0, HALF)
         gather(5, HALF, V)
+        quantize(0, 0, V, "table5")
+        gather(6, 0, HALF)
+        gather(6, HALF, V)
         gather(7, 0, HALF)
         gather(7, HALF, V)
         interleave_w(sc, 0, 0)

@@ -76,12 +76,8 @@ def tile_picked_grid_lin_none_sub_l_kernel(tc, xT, w, offs, out):
         load_w(1, 0, 1)
         load_w(1, 1, 2)
 
-        spans = {0: [(0, V)], 1: [(0, HALF), (HALF, V)]}
-        pairs = {}
+        pairs = [keep.tile([P, PACK * V], BF16, name=f"pairs{g}", align_bytes=64) for g in range(PASSES)]
         grouped = {}
-        for g in range(PASSES):
-            for v0, v1 in spans[g]:
-                pairs[g, v0] = keep.tile([P, 2, v1 - v0, 2], BF16, name=f"pairs{g}_{v0}", align_bytes=64)
         codes = {}
         scales = {}
         w_grouped = {}
@@ -97,23 +93,26 @@ def tile_picked_grid_lin_none_sub_l_kernel(tc, xT, w, offs, out):
 
         def gather(l, v0, v1):
             g, j = divmod(l, PACK)
-            dst = pairs[g, v0][:, j // 2, :, j % 2]
+            dst = pairs[g][:].rearrange("p (a v e) -> p a v e", a=2, e=2)[:, j // 2, v0:v1, j % 2]
             if j < 2:
                 nc.scalar.activation(dst, narrow[l][:].indirect(listed(l, v0, v1)), COPY)
             else:
                 nc.vector.tensor_copy(dst, tables[l].indirect(listed(l, v0, v1)))
 
         def weave(copy, word, g, v0, v1, tag):
-            grouped[g, v0] = keep.tile([P, (v1 - v0) * PACK], BF16, name=f"grouped{g}_{v0}", tag=tag, align_bytes=64)
+            dst = keep.tile([P, (v1 - v0) * PACK], BF16, name=f"grouped{g}_{v0}", tag=tag, align_bytes=64)[:]
+            words = pairs[g][:].bitcast(word).rearrange("p (a v) -> p a v", a=2)
             copy(
-                out=grouped[g, v0][:].bitcast(word).rearrange("p (v a) -> p v a", a=2),
-                in_=pairs[g, v0][:].rearrange("p a v e -> p a (v e)").bitcast(word).rearrange("p a v -> p v a"),
+                out=dst.bitcast(word).rearrange("p (v a) -> p v a", a=2),
+                in_=words[:, :, v0:v1].rearrange("p a v -> p v a"),
             )
+            for c0 in range(v0, v1, HALF):
+                grouped[g, c0] = dst[:, (c0 - v0) * PACK : (c0 - v0 + HALF) * PACK]
 
         def quantize(g, v0, v1, tag):
             words = keep.tile([P, v1 - v0], U32, name=f"codes{g}_{v0}", tag=tag, align_bytes=64)
             plane = keep.tile([P, v1 - v0], U8, name=f"scales{g}_{v0}", align_bytes=64)
-            nc.vector.quantize_mx(out=words[:].bitcast(FP8X4), scales=plane[:], in_=grouped[g, v0][:])
+            nc.vector.quantize_mx(out=words[:].bitcast(FP8X4), scales=plane[:], in_=grouped[g, v0])
             for c0 in range(v0, v1, HALF):
                 codes[g, c0 // HALF] = words[:, c0 - v0 : c0 - v0 + HALF]
                 scales[g, c0 // HALF] = plane[:, c0 - v0 : c0 - v0 + HALF]
@@ -151,30 +150,30 @@ def tile_picked_grid_lin_none_sub_l_kernel(tc, xT, w, offs, out):
         gather(2, 0, V)
         cast(vc, 1)
         gather(1, 0, V)
-        gather(3, 0, V)
-        weave(sc, U32, 0, 0, V, "grouped0")
-        cast(vc, 4)
-        gather(4, 0, HALF)
-        gather(4, HALF, V)
+        gather(3, 0, HALF)
+        gather(3, HALF, V)
+        cast(sc, 4)
+        gather(4, 0, V)
+        weave(vc, I32, 0, 0, HALF, "grouped0a")
+        weave(vc, I32, 0, HALF, V, "grouped0b")
+        quantize(0, 0, HALF, "codes0a")
+        quantize(0, HALF, V, "codes0b")
         cast(vc, 5)
-        gather(5, 0, HALF)
-        gather(5, HALF, V)
-        quantize(0, 0, V, "table5")
-        gather(6, 0, HALF)
-        gather(6, HALF, V)
+        gather(5, 0, V)
+        gather(6, 0, V)
         gather(7, 0, HALF)
         gather(7, HALF, V)
+        weave(vc, I32, 1, 0, HALF, "grouped1a")
         interleave_w(sc, 0, 0)
         quantize_w(0, 0)
         multiply(0, 0, 0)
         multiply(0, 0, 1)
-        weave(vc, I32, 1, 0, HALF, "w_raw00")
+        weave(vc, I32, 1, HALF, V, "w_raw00")
         interleave_w(sc, 0, 1)
         quantize_w(0, 1)
         multiply(0, 1, 0)
         multiply(0, 1, 1)
-        weave(vc, I32, 1, HALF, V, "w_raw01")
-        quantize(1, 0, HALF, "w_grouped01")
+        quantize(1, 0, HALF, "w_raw01")
         interleave_w(sc, 1, 0)
         quantize_w(1, 0)
         quantize(1, HALF, V, "w_raw10")

@@ -157,8 +157,20 @@ def tile_picked_grid_lin_none_sub_l_kernel(tc, xT, w, offs, out):
         weave(vc, I32, 0, 0, HALF, "grouped0a")
         weave(vc, I32, 0, HALF, V, "grouped0b")
         quantize(0, 0, HALF, "codes0a")
-        quantize(0, HALF, V, "codes0b")
         cast(vc, 5)
+        quantize(0, HALF, V, "table4")
+        spin = psum.tile([32, 4, P], F32, name="spin")
+        for i in range(16):
+            cols = slice(i % 2 * P, (i % 2 + 1) * P)
+            nc.tensor.matmul_mx(
+                out=spin[:, i % 4, :],
+                lhsT=codes[0, 1][:, 0:32].bitcast(FP8X4),
+                lhsT_scale=scales[0, 1][:, 0:32],
+                rhs=codes[0, 1][:, cols].bitcast(FP8X4),
+                rhs_scale=scales[0, 1][:, cols],
+                start=True,
+                stop=True,
+            )
         gather(5, 0, V)
         gather(6, 0, V)
         gather(7, 0, HALF)

@@ -72,8 +72,8 @@ def tile_picked_grid_lin_none_sub_l_kernel(tc, xT, w, offs, out):
         load_level(6)
         load_level(7)
         load_w(0, 0, 1)
-        load_w(0, 1, 2)
         load_w(1, 0, 1)
+        load_w(0, 1, 2)
         load_w(1, 1, 2)
 
         pairs = [keep.tile([P, PACK * V], BF16, name=f"pairs{g}", align_bytes=64) for g in range(PASSES)]
@@ -89,7 +89,6 @@ def tile_picked_grid_lin_none_sub_l_kernel(tc, xT, w, offs, out):
                 w_codes[g, m] = keep.tile([P, P], U32, name=f"w_codes{g}{m}", align_bytes=64)
                 w_scales[g, m] = keep.tile([P, P], U8, name=f"w_scales{g}{m}", align_bytes=64)
         acc = [[psum.tile([P, HALF], F32, name=f"acc{m}{c}") for c in range(2)] for m in range(2)]
-        res = [[keep.tile([P, HALF], F32, name=f"res{m}{c}", align_bytes=64) for c in range(2)] for m in range(2)]
 
         def gather(l, v0, v1):
             g, j = divmod(l, PACK)
@@ -141,9 +140,10 @@ def tile_picked_grid_lin_none_sub_l_kernel(tc, xT, w, offs, out):
                 stop=(g == PASSES - 1),
             )
 
-        def store(copy, queue, m, c):
-            copy(out=res[m][c][:], in_=acc[m][c][:])
-            queue.dma_start(out=out[m * P : (m + 1) * P, c * HALF : (c + 1) * HALF], in_=res[m][c][:])
+        def store(copy, queue, m, c, tag):
+            res = keep.tile([P, HALF], F32, name=f"res{m}{c}", tag=tag, align_bytes=64)
+            copy(out=res[:], in_=acc[m][c][:])
+            queue.dma_start(out=out[m * P : (m + 1) * P, c * HALF : (c + 1) * HALF], in_=res[:])
 
         cast(vc, 0)
         gather(0, 0, V)
@@ -181,21 +181,21 @@ def tile_picked_grid_lin_none_sub_l_kernel(tc, xT, w, offs, out):
         multiply(0, 0, 0)
         multiply(0, 0, 1)
         weave(vc, I32, 1, HALF, V, "w_raw00")
+        quantize(1, 0, HALF, "w_grouped00")
+        interleave_w(sc, 1, 0)
+        quantize_w(1, 0)
+        multiply(1, 0, 0)
+        quantize(1, HALF, V, "w_raw10")
+        multiply(1, 0, 1)
         interleave_w(sc, 0, 1)
         quantize_w(0, 1)
         multiply(0, 1, 0)
         multiply(0, 1, 1)
-        quantize(1, 0, HALF, "w_raw01")
-        interleave_w(sc, 1, 0)
-        quantize_w(1, 0)
-        quantize(1, HALF, V, "w_raw10")
-        multiply(1, 0, 0)
-        multiply(1, 0, 1)
         interleave_w(sc, 1, 1)
         quantize_w(1, 1)
         multiply(1, 1, 0)
         multiply(1, 1, 1)
-        store(sc, nc.scalar, 0, 0)
-        store(vc, nc.sync, 0, 1)
-        store(sc, nc.scalar, 1, 0)
-        store(vc, nc.sync, 1, 1)
+        store(sc, nc.scalar, 0, 0, "w_raw11")
+        store(vc, nc.sync, 0, 1, "w_grouped11")
+        store(sc, nc.scalar, 1, 0, "res10")
+        store(vc, nc.sync, 1, 1, "res11")

@@ -160,11 +160,13 @@ def tile_picked_grid_lin_none_sub_l_kernel(tc, xT, w, offs, out):
         cast(vc, 5)
         quantize(0, HALF, V, "table4")
         spin = psum.tile([32, 4, P], F32, name="spin")
+        spin_codes = keep.tile([P, 32], U32, name="spin_codes", align_bytes=64)
+        nc.gpsimd.tensor_copy(spin_codes[:], codes[0, 1][:, 0:32])
         for i in range(16):
             cols = slice(i % 2 * P, (i % 2 + 1) * P)
             nc.tensor.matmul_mx(
                 out=spin[:, i % 4, :],
-                lhsT=codes[0, 1][:, 0:32].bitcast(FP8X4),
+                lhsT=spin_codes[:].bitcast(FP8X4),
                 lhsT_scale=scales[0, 1][:, 0:32],
                 rhs=codes[0, 1][:, cols].bitcast(FP8X4),
                 rhs_scale=scales[0, 1][:, cols],

@@ -193,7 +193,12 @@ def tile_picked_grid_lin_none_sub_l_kernel(tc, xT, w, offs, out):
         quantize_w(0, 1)
         multiply(0, 1, 0)
         multiply(0, 1, 1)
-        interleave_w(sc, 1, 1)
+        for h, copy in enumerate((sc, vc)):
+            cols = slice(h * P // 2, (h + 1) * P // 2)
+            copy(
+                out=w_grouped[1, 1][:, cols, :].rearrange("p (c i) j -> p c j i", i=4),
+                in_=w_raw[1, 1][:, :, cols].rearrange("p j (c i) -> p c j i", i=4),
+            )
         quantize_w(1, 1)
         multiply(1, 1, 0)
         multiply(1, 1, 1)

@@ -62,10 +62,12 @@ def tile_picked_grid_lin_none_sub_l_kernel(tc, xT, w, offs, out):
             narrow[l] = keep.tile([P, T], BF16, name=f"narrow{l}", align_bytes=64)
             copy(out=narrow[l][:], in_=tables[l])
 
-        load_level(0)
+        first = keep.tile([P, 2 * T], F32, name="first", align_bytes=64)
+        nc.sync.dma_start(out=first[:], in_=xT[0:K_PASS, :].rearrange("(p j) t -> p (j t)", j=PACK)[:, 0 : 2 * T])
+        tables[0] = first[:, 0:T]
+        tables[1] = first[:, T : 2 * T]
         nc.sync.dma_start(offsets[:], offs)
         load_level(2)
-        load_level(1)
         load_level(3)
         load_level(4)
         load_level(5)
@@ -147,9 +149,9 @@ def tile_picked_grid_lin_none_sub_l_kernel(tc, xT, w, offs, out):
 
         cast(vc, 0)
         gather(0, 0, V)
-        gather(2, 0, V)
         cast(vc, 1)
         gather(1, 0, V)
+        gather(2, 0, V)
         gather(3, 0, HALF)
         gather(3, HALF, V)
         cast(sc, 4)
@@ -193,8 +195,7 @@ def tile_picked_grid_lin_none_sub_l_kernel(tc, xT, w, offs, out):
         quantize_w(0, 1)
         multiply(0, 1, 0)
         multiply(0, 1, 1)
-        for h, copy in enumerate((sc, vc)):
-            cols = slice(h * P // 2, (h + 1) * P // 2)
+        for copy, cols in ((sc, slice(0, 96)), (vc, slice(96, P))):
             copy(
                 out=w_grouped[1, 1][:, cols, :].rearrange("p (c i) j -> p c j i", i=4),
                 in_=w_raw[1, 1][:, :, cols].rearrange("p j (c i) -> p c j i", i=4),

@@ -19,7 +19,11 @@ P = 128
 PACK = 4
 K_PASS = P * PACK
 PASSES = K // K_PASS
+ROW_TILES = N // P
 HALF = V // 2
+LIST_ROWS = 16
+LINE = 4
+SCALAR_COLS = 96
 
 
 def tile_picked_grid_lin_none_sub_l_kernel(tc, xT, w, offs, out):
@@ -28,100 +32,78 @@ def tile_picked_grid_lin_none_sub_l_kernel(tc, xT, w, offs, out):
         keep = ctx.enter_context(tc.tile_pool(name="keep", bufs=1))
         psum = ctx.enter_context(tc.psum_pool(name="psum", bufs=1))
 
-        offsets = keep.tile([P, D * V // 16], U16, name="offsets")
+        offsets = keep.tile([P, D * V // LIST_ROWS], U16, name="offsets")
 
         warm = keep.tile([P, 1], F32, name="warm")
         warm_out = keep.tile([P, 1], F32, name="warm_out")
         nc.vector.memset(warm[:], 0.0)
         nc.scalar.activation(warm_out[:], warm[:], COPY)
 
-        sc, vc = nc.scalar.copy, nc.vector.tensor_copy
-        tables = {}
-        w_raw = {}
-        narrow = {}
+        on_scalar, on_vector = nc.scalar.copy, nc.vector.tensor_copy
 
-        def load_level(l):
+        first = keep.tile([P, 2 * T], F32, name="first", align_bytes=64)
+        nc.sync.dma_start(out=first[:], in_=xT[0:K_PASS, :].rearrange("(p j) t -> p (j t)", j=PACK)[:, 0 : 2 * T])
+        tables = {0: first[:, 0:T], 1: first[:, T : 2 * T]}
+        nc.sync.dma_start(offsets[:], offs)
+        for l in range(2, D):
             g, j = divmod(l, PACK)
             table = keep.tile([P, T], F32, name=f"table{l}", align_bytes=64)
             rows = xT[g * K_PASS : (g + 1) * K_PASS, :].rearrange("(p j) t -> p j t", j=PACK)
             nc.sync.dma_start(out=table[:], in_=rows[:, j, :])
             tables[l] = table[:]
-
-        def load_w(g, m0, m1):
-            raw = keep.tile([P, PACK, (m1 - m0) * P], F32, name=f"w_raw{g}{m0}", align_bytes=64)
-            rows = w[g * K_PASS : (g + 1) * K_PASS, m0 * P : m1 * P].rearrange("(p j) n -> p j n", j=PACK)
-            nc.sync.dma_start(out=raw[:], in_=rows)
-            for m in range(m0, m1):
-                w_raw[g, m] = raw[:, :, (m - m0) * P : (m - m0 + 1) * P]
-
-        def listed(l, v0, v1):
-            c0 = l * V // 16
-            return offsets[:, c0 + v0 // 16 : c0 + v1 // 16]
-
-        def cast(copy, l):
-            narrow[l] = keep.tile([P, T], BF16, name=f"narrow{l}", align_bytes=64)
-            copy(out=narrow[l][:], in_=tables[l])
-
-        first = keep.tile([P, 2 * T], F32, name="first", align_bytes=64)
-        nc.sync.dma_start(out=first[:], in_=xT[0:K_PASS, :].rearrange("(p j) t -> p (j t)", j=PACK)[:, 0 : 2 * T])
-        tables[0] = first[:, 0:T]
-        tables[1] = first[:, T : 2 * T]
-        nc.sync.dma_start(offsets[:], offs)
-        load_level(2)
-        load_level(3)
-        load_level(4)
-        load_level(5)
-        load_level(6)
-        load_level(7)
-        load_w(0, 0, 1)
-        load_w(1, 0, 1)
-        load_w(0, 1, 2)
-        load_w(1, 1, 2)
+        w_raw = {}
+        for m in range(ROW_TILES):
+            for g in range(PASSES):
+                w_raw[g, m] = keep.tile([P, PACK, P], F32, name=f"w_raw{g}{m}", align_bytes=64)
+                rows = w[g * K_PASS : (g + 1) * K_PASS, m * P : (m + 1) * P].rearrange("(p j) n -> p j n", j=PACK)
+                nc.sync.dma_start(out=w_raw[g, m][:], in_=rows)
 
         pairs = [keep.tile([P, PACK * V], BF16, name=f"pairs{g}", align_bytes=64) for g in range(PASSES)]
-        grouped = {}
+        narrow = {}
+        woven = {}
         codes = {}
         scales = {}
         w_grouped = {}
         w_codes = {}
         w_scales = {}
         for g in range(PASSES):
-            for m in range(2):
+            for m in range(ROW_TILES):
                 w_grouped[g, m] = keep.tile([P, P, PACK], BF16, name=f"w_grouped{g}{m}", align_bytes=64)
                 w_codes[g, m] = keep.tile([P, P], U32, name=f"w_codes{g}{m}", align_bytes=64)
                 w_scales[g, m] = keep.tile([P, P], U8, name=f"w_scales{g}{m}", align_bytes=64)
-        acc = [[psum.tile([P, HALF], F32, name=f"acc{m}{c}") for c in range(2)] for m in range(2)]
+        acc = [[psum.tile([P, HALF], F32, name=f"acc{m}{c}") for c in range(2)] for m in range(ROW_TILES)]
+
+
+        def cast(copy, l):
+            narrow[l] = keep.tile([P, T], BF16, name=f"narrow{l}", align_bytes=64)
+            copy(out=narrow[l][:], in_=tables[l])
 
         def gather(l, v0, v1):
             g, j = divmod(l, PACK)
             dst = pairs[g][:].rearrange("p (a v e) -> p a v e", a=2, e=2)[:, j // 2, v0:v1, j % 2]
+            entries = offsets[:, (l * V + v0) // LIST_ROWS : (l * V + v1) // LIST_ROWS]
             if j < 2:
-                nc.scalar.activation(dst, narrow[l][:].indirect(listed(l, v0, v1)), COPY)
+                nc.scalar.activation(dst, narrow[l][:].indirect(entries), COPY)
             else:
-                nc.vector.tensor_copy(dst, tables[l].indirect(listed(l, v0, v1)))
+                nc.vector.tensor_copy(dst, tables[l].indirect(entries))
 
-        def weave(copy, word, g, v0, v1, tag):
-            dst = keep.tile([P, (v1 - v0) * PACK], BF16, name=f"grouped{g}_{v0}", tag=tag, align_bytes=64)[:]
-            words = pairs[g][:].bitcast(word).rearrange("p (a v) -> p a v", a=2)
-            copy(
-                out=dst.bitcast(word).rearrange("p (v a) -> p v a", a=2),
-                in_=words[:, :, v0:v1].rearrange("p a v -> p v a"),
+        def weave(g, c, tag):
+            woven[g, c] = keep.tile([P, HALF * PACK], BF16, name=f"woven{g}{c}", tag=tag, align_bytes=64)
+            words = pairs[g][:].bitcast(I32).rearrange("p (a v) -> p a v", a=2)
+            nc.vector.tensor_copy(
+                out=woven[g, c][:].bitcast(I32).rearrange("p (v a) -> p v a", a=2),
+                in_=words[:, :, c * HALF : (c + 1) * HALF].rearrange("p a v -> p v a"),
             )
-            for c0 in range(v0, v1, HALF):
-                grouped[g, c0] = dst[:, (c0 - v0) * PACK : (c0 - v0 + HALF) * PACK]
 
-        def quantize(g, v0, v1, tag):
-            words = keep.tile([P, v1 - v0], U32, name=f"codes{g}_{v0}", tag=tag, align_bytes=64)
-            plane = keep.tile([P, v1 - v0], U8, name=f"scales{g}_{v0}", align_bytes=64)
-            nc.vector.quantize_mx(out=words[:].bitcast(FP8X4), scales=plane[:], in_=grouped[g, v0])
-            for c0 in range(v0, v1, HALF):
-                codes[g, c0 // HALF] = words[:, c0 - v0 : c0 - v0 + HALF]
-                scales[g, c0 // HALF] = plane[:, c0 - v0 : c0 - v0 + HALF]
+        def quantize_x(g, c, tag):
+            codes[g, c] = keep.tile([P, HALF], U32, name=f"codes{g}{c}", tag=tag, align_bytes=64)
+            scales[g, c] = keep.tile([P, HALF], U8, name=f"scales{g}{c}", align_bytes=64)
+            nc.vector.quantize_mx(out=codes[g, c][:].bitcast(FP8X4), scales=scales[g, c][:], in_=woven[g, c][:])
 
-        def interleave_w(copy, g, m):
+        def interleave_w(copy, g, m, n0, n1):
             copy(
-                out=w_grouped[g, m][:].rearrange("p (c i) j -> p c j i", i=4),
-                in_=w_raw[g, m].rearrange("p j (c i) -> p c j i", i=4),
+                out=w_grouped[g, m][:, n0:n1, :].rearrange("p (b i) j -> p b j i", i=LINE),
+                in_=w_raw[g, m][:, :, n0:n1].rearrange("p j (b i) -> p b j i", i=LINE),
             )
 
         def quantize_w(g, m):
@@ -136,8 +118,8 @@ def tile_picked_grid_lin_none_sub_l_kernel(tc, xT, w, offs, out):
                 out=acc[m][c][:],
                 lhsT=w_codes[g, m][:].bitcast(FP8X4),
                 lhsT_scale=w_scales[g, m][:],
-                rhs=codes[g, c].bitcast(FP8X4),
-                rhs_scale=scales[g, c],
+                rhs=codes[g, c][:].bitcast(FP8X4),
+                rhs_scale=scales[g, c][:],
                 start=(g == 0),
                 stop=(g == PASSES - 1),
             )
@@ -147,63 +129,50 @@ def tile_picked_grid_lin_none_sub_l_kernel(tc, xT, w, offs, out):
             copy(out=res[:], in_=acc[m][c][:])
             queue.dma_start(out=out[m * P : (m + 1) * P, c * HALF : (c + 1) * HALF], in_=res[:])
 
-        cast(vc, 0)
+        cast(on_vector, 0)
         gather(0, 0, V)
-        cast(vc, 1)
+        cast(on_vector, 1)
         gather(1, 0, V)
         gather(2, 0, V)
         gather(3, 0, HALF)
         gather(3, HALF, V)
-        cast(sc, 4)
+        weave(0, 0, "woven00")
+        weave(0, 1, "woven01")
+        quantize_x(0, 0, "codes00")
+        quantize_x(0, 1, "codes01")
+
+        cast(on_scalar, 4)
         gather(4, 0, V)
-        weave(vc, I32, 0, 0, HALF, "grouped0a")
-        weave(vc, I32, 0, HALF, V, "grouped0b")
-        quantize(0, 0, HALF, "codes0a")
-        cast(vc, 5)
-        quantize(0, HALF, V, "table4")
-        spin = psum.tile([32, 4, P], F32, name="spin")
-        spin_codes = keep.tile([P, 32], U32, name="spin_codes", align_bytes=64)
-        nc.gpsimd.tensor_copy(spin_codes[:], codes[0, 1][:, 0:32])
-        for i in range(16):
-            cols = slice(i % 2 * P, (i % 2 + 1) * P)
-            nc.tensor.matmul_mx(
-                out=spin[:, i % 4, :],
-                lhsT=spin_codes[:].bitcast(FP8X4),
-                lhsT_scale=scales[0, 1][:, 0:32],
-                rhs=codes[0, 1][:, cols].bitcast(FP8X4),
-                rhs_scale=scales[0, 1][:, cols],
-                start=True,
-                stop=True,
-            )
+        cast(on_vector, 5)
         gather(5, 0, V)
         gather(6, 0, V)
         gather(7, 0, HALF)
         gather(7, HALF, V)
-        weave(vc, I32, 1, 0, HALF, "grouped1a")
-        interleave_w(sc, 0, 0)
+
+        weave(1, 0, "woven10")
+        interleave_w(on_scalar, 0, 0, 0, P)
         quantize_w(0, 0)
         multiply(0, 0, 0)
         multiply(0, 0, 1)
-        weave(vc, I32, 1, HALF, V, "w_raw00")
-        quantize(1, 0, HALF, "w_grouped00")
-        interleave_w(sc, 1, 0)
+        weave(1, 1, "w_raw00")
+        quantize_x(1, 0, "w_grouped00")
+        interleave_w(on_scalar, 1, 0, 0, P)
         quantize_w(1, 0)
         multiply(1, 0, 0)
-        quantize(1, HALF, V, "w_raw10")
+        quantize_x(1, 1, "w_raw10")
         multiply(1, 0, 1)
-        interleave_w(sc, 0, 1)
+
+        interleave_w(on_scalar, 0, 1, 0, P)
         quantize_w(0, 1)
         multiply(0, 1, 0)
         multiply(0, 1, 1)
-        for copy, cols in ((sc, slice(0, 96)), (vc, slice(96, P))):
-            copy(
-                out=w_grouped[1, 1][:, cols, :].rearrange("p (c i) j -> p c j i", i=4),
-                in_=w_raw[1, 1][:, :, cols].rearrange("p j (c i) -> p c j i", i=4),
-            )
+        interleave_w(on_scalar, 1, 1, 0, SCALAR_COLS)
+        interleave_w(on_vector, 1, 1, SCALAR_COLS, P)
         quantize_w(1, 1)
         multiply(1, 1, 0)
         multiply(1, 1, 1)
-        store(sc, nc.scalar, 0, 0, "w_raw11")
-        store(vc, nc.sync, 0, 1, "w_grouped11")
-        store(sc, nc.scalar, 1, 0, "res10")
-        store(vc, nc.sync, 1, 1, "res11")
+
+        store(on_scalar, nc.scalar, 0, 0, "w_raw11")
+        store(on_vector, nc.sync, 0, 1, "w_grouped11")
+        store(on_scalar, nc.scalar, 1, 0, "res10")
+        store(on_vector, nc.sync, 1, 1, "res11")

@@ -41,24 +41,24 @@ def tile_picked_grid_lin_none_sub_l_kernel(tc, xT, w, offs, out):
 
         on_scalar, on_vector = nc.scalar.copy, nc.vector.tensor_copy
 
-        first = keep.tile([P, 2 * T], F32, name="first", align_bytes=64)
+        first = keep.tile([P, 2 * T], F32, name="first", align_bytes=256)
         nc.sync.dma_start(out=first[:], in_=xT[0:K_PASS, :].rearrange("(p j) t -> p (j t)", j=PACK)[:, 0 : 2 * T])
         tables = {0: first[:, 0:T], 1: first[:, T : 2 * T]}
         nc.sync.dma_start(offsets[:], offs)
         for l in range(2, D):
             g, j = divmod(l, PACK)
-            table = keep.tile([P, T], F32, name=f"table{l}", align_bytes=64)
+            table = keep.tile([P, T], F32, name=f"table{l}", align_bytes=256)
             rows = xT[g * K_PASS : (g + 1) * K_PASS, :].rearrange("(p j) t -> p j t", j=PACK)
             nc.sync.dma_start(out=table[:], in_=rows[:, j, :])
             tables[l] = table[:]
         w_raw = {}
         for m in range(ROW_TILES):
             for g in range(PASSES):
-                w_raw[g, m] = keep.tile([P, PACK, P], F32, name=f"w_raw{g}{m}", align_bytes=64)
+                w_raw[g, m] = keep.tile([P, PACK, P], F32, name=f"w_raw{g}{m}", align_bytes=256)
                 rows = w[g * K_PASS : (g + 1) * K_PASS, m * P : (m + 1) * P].rearrange("(p j) n -> p j n", j=PACK)
                 nc.sync.dma_start(out=w_raw[g, m][:], in_=rows)
 
-        pairs = [keep.tile([P, PACK * V], BF16, name=f"pairs{g}", align_bytes=64) for g in range(PASSES)]
+        pairs = [keep.tile([P, PACK * V], BF16, name=f"pairs{g}", align_bytes=256) for g in range(PASSES)]
         narrow = {}
         woven = {}
         codes = {}
@@ -68,14 +68,14 @@ def tile_picked_grid_lin_none_sub_l_kernel(tc, xT, w, offs, out):
         w_scales = {}
         for g in range(PASSES):
             for m in range(ROW_TILES):
-                w_grouped[g, m] = keep.tile([P, P, PACK], BF16, name=f"w_grouped{g}{m}", align_bytes=64)
-                w_codes[g, m] = keep.tile([P, P], U32, name=f"w_codes{g}{m}", align_bytes=64)
-                w_scales[g, m] = keep.tile([P, P], U8, name=f"w_scales{g}{m}", align_bytes=64)
+                w_grouped[g, m] = keep.tile([P, P, PACK], BF16, name=f"w_grouped{g}{m}", align_bytes=256)
+                w_codes[g, m] = keep.tile([P, P], U32, name=f"w_codes{g}{m}", align_bytes=256)
+                w_scales[g, m] = keep.tile([P, P], U8, name=f"w_scales{g}{m}", align_bytes=256)
         acc = [[psum.tile([P, HALF], F32, name=f"acc{m}{c}") for c in range(2)] for m in range(ROW_TILES)]
 
 
         def cast(copy, l):
-            narrow[l] = keep.tile([P, T], BF16, name=f"narrow{l}", align_bytes=64)
+            narrow[l] = keep.tile([P, T], BF16, name=f"narrow{l}", align_bytes=256)
             copy(out=narrow[l][:], in_=tables[l])
 
         def gather(l, v0, v1):
@@ -88,7 +88,7 @@ def tile_picked_grid_lin_none_sub_l_kernel(tc, xT, w, offs, out):
                 nc.vector.tensor_copy(dst, tables[l].indirect(entries))
 
         def weave(g, c, tag):
-            woven[g, c] = keep.tile([P, HALF * PACK], BF16, name=f"woven{g}{c}", tag=tag, align_bytes=64)
+            woven[g, c] = keep.tile([P, HALF * PACK], BF16, name=f"woven{g}{c}", tag=tag, align_bytes=256)
             words = pairs[g][:].bitcast(I32).rearrange("p (a v) -> p a v", a=2)
             nc.vector.tensor_copy(
                 out=woven[g, c][:].bitcast(I32).rearrange("p (v a) -> p v a", a=2),
@@ -96,8 +96,8 @@ def tile_picked_grid_lin_none_sub_l_kernel(tc, xT, w, offs, out):
             )
 
         def quantize_x(g, c, tag):
-            codes[g, c] = keep.tile([P, HALF], U32, name=f"codes{g}{c}", tag=tag, align_bytes=64)
-            scales[g, c] = keep.tile([P, HALF], U8, name=f"scales{g}{c}", align_bytes=64)
+            codes[g, c] = keep.tile([P, HALF], U32, name=f"codes{g}{c}", tag=tag, align_bytes=256)
+            scales[g, c] = keep.tile([P, HALF], U8, name=f"scales{g}{c}", align_bytes=256)
             nc.vector.quantize_mx(out=codes[g, c][:].bitcast(FP8X4), scales=scales[g, c][:], in_=woven[g, c][:])
 
         def interleave_w(copy, g, m, n0, n1):
@@ -125,7 +125,7 @@ def tile_picked_grid_lin_none_sub_l_kernel(tc, xT, w, offs, out):
             )
 
         def store(copy, queue, m, c, tag):
-            res = keep.tile([P, HALF], F32, name=f"res{m}{c}", tag=tag, align_bytes=64)
+            res = keep.tile([P, HALF], F32, name=f"res{m}{c}", tag=tag, align_bytes=256)
             copy(out=res[:], in_=acc[m][c][:])
             queue.dma_start(out=out[m * P : (m + 1) * P, c * HALF : (c + 1) * HALF], in_=res[:])
 

@@ -23,7 +23,6 @@ ROW_TILES = N // P
 HALF = V // 2
 LIST_ROWS = 16
 LINE = 4
-SCALAR_COLS = 96
 
 
 def tile_picked_grid_lin_none_sub_l_kernel(tc, xT, w, offs, out):
@@ -32,7 +31,7 @@ def tile_picked_grid_lin_none_sub_l_kernel(tc, xT, w, offs, out):
         keep = ctx.enter_context(tc.tile_pool(name="keep", bufs=1))
         psum = ctx.enter_context(tc.psum_pool(name="psum", bufs=1))
 
-        offsets = keep.tile([P, D * V // LIST_ROWS], U16, name="offsets")
+        offsets = keep.tile([P, D * V // LIST_ROWS], U16, name="offsets", align_bytes=256)
 
         warm = keep.tile([P, 1], F32, name="warm")
         warm_out = keep.tile([P, 1], F32, name="warm_out")
@@ -113,15 +112,15 @@ def tile_picked_grid_lin_none_sub_l_kernel(tc, xT, w, offs, out):
                 in_=w_grouped[g, m][:].rearrange("p n j -> p (n j)"),
             )
 
-        def multiply(g, m, c):
+        def multiply(g, m, c, opens):
             nc.tensor.matmul_mx(
                 out=acc[m][c][:],
                 lhsT=w_codes[g, m][:].bitcast(FP8X4),
                 lhsT_scale=w_scales[g, m][:],
                 rhs=codes[g, c][:].bitcast(FP8X4),
                 rhs_scale=scales[g, c][:],
-                start=(g == 0),
-                stop=(g == PASSES - 1),
+                start=opens,
+                stop=not opens,
             )
 
         def store(copy, queue, m, c, tag):
@@ -152,25 +151,24 @@ def tile_picked_grid_lin_none_sub_l_kernel(tc, xT, w, offs, out):
         weave(1, 0, "woven10")
         interleave_w(on_scalar, 0, 0, 0, P)
         quantize_w(0, 0)
-        multiply(0, 0, 0)
-        multiply(0, 0, 1)
+        multiply(0, 0, 0, True)
+        multiply(0, 0, 1, True)
         weave(1, 1, "w_raw00")
         quantize_x(1, 0, "w_grouped00")
         interleave_w(on_scalar, 1, 0, 0, P)
         quantize_w(1, 0)
-        multiply(1, 0, 0)
+        multiply(1, 0, 0, False)
         quantize_x(1, 1, "w_raw10")
-        multiply(1, 0, 1)
+        multiply(1, 0, 1, False)
 
         interleave_w(on_scalar, 0, 1, 0, P)
         quantize_w(0, 1)
-        multiply(0, 1, 0)
-        multiply(0, 1, 1)
-        interleave_w(on_scalar, 1, 1, 0, SCALAR_COLS)
-        interleave_w(on_vector, 1, 1, SCALAR_COLS, P)
+        multiply(0, 1, 0, True)
+        interleave_w(on_scalar, 1, 1, 0, P)
         quantize_w(1, 1)
-        multiply(1, 1, 0)
-        multiply(1, 1, 1)
+        multiply(1, 1, 0, False)
+        multiply(1, 1, 1, True)
+        multiply(0, 1, 1, False)
 
         store(on_scalar, nc.scalar, 0, 0, "w_raw11")
         store(on_vector, nc.sync, 0, 1, "w_grouped11")

@@ -31,7 +31,7 @@ def tile_picked_grid_lin_none_sub_l_kernel(tc, xT, w, offs, out):
         keep = ctx.enter_context(tc.tile_pool(name="keep", bufs=1))
         psum = ctx.enter_context(tc.psum_pool(name="psum", bufs=1))
 
-        offsets = keep.tile([P, D * V // LIST_ROWS], U16, name="offsets", align_bytes=256)
+        offsets = keep.tile([P, D * V // LIST_ROWS], U16, name="offsets", align_bytes=512)
 
         warm = keep.tile([P, 1], F32, name="warm")
         warm_out = keep.tile([P, 1], F32, name="warm_out")
@@ -40,24 +40,24 @@ def tile_picked_grid_lin_none_sub_l_kernel(tc, xT, w, offs, out):
 
         on_scalar, on_vector = nc.scalar.copy, nc.vector.tensor_copy
 
-        first = keep.tile([P, 2 * T], F32, name="first", align_bytes=256)
+        first = keep.tile([P, 2 * T], F32, name="first", align_bytes=512)
         nc.sync.dma_start(out=first[:], in_=xT[0:K_PASS, :].rearrange("(p j) t -> p (j t)", j=PACK)[:, 0 : 2 * T])
         tables = {0: first[:, 0:T], 1: first[:, T : 2 * T]}
         nc.sync.dma_start(offsets[:], offs)
         for l in range(2, D):
             g, j = divmod(l, PACK)
-            table = keep.tile([P, T], F32, name=f"table{l}", align_bytes=256)
+            table = keep.tile([P, T], F32, name=f"table{l}", align_bytes=512)
             rows = xT[g * K_PASS : (g + 1) * K_PASS, :].rearrange("(p j) t -> p j t", j=PACK)
             nc.sync.dma_start(out=table[:], in_=rows[:, j, :])
             tables[l] = table[:]
         w_raw = {}
         for m in range(ROW_TILES):
             for g in range(PASSES):
-                w_raw[g, m] = keep.tile([P, PACK, P], F32, name=f"w_raw{g}{m}", align_bytes=256)
+                w_raw[g, m] = keep.tile([P, PACK, P], F32, name=f"w_raw{g}{m}", align_bytes=512)
                 rows = w[g * K_PASS : (g + 1) * K_PASS, m * P : (m + 1) * P].rearrange("(p j) n -> p j n", j=PACK)
                 nc.sync.dma_start(out=w_raw[g, m][:], in_=rows)
 
-        pairs = [keep.tile([P, PACK * V], BF16, name=f"pairs{g}", align_bytes=256) for g in range(PASSES)]
+        pairs = [keep.tile([P, PACK * V], BF16, name=f"pairs{g}", align_bytes=512) for g in range(PASSES)]
         narrow = {}
         woven = {}
         codes = {}
@@ -67,14 +67,14 @@ def tile_picked_grid_lin_none_sub_l_kernel(tc, xT, w, offs, out):
         w_scales = {}
         for g in range(PASSES):
             for m in range(ROW_TILES):
-                w_grouped[g, m] = keep.tile([P, P, PACK], BF16, name=f"w_grouped{g}{m}", align_bytes=256)
-                w_codes[g, m] = keep.tile([P, P], U32, name=f"w_codes{g}{m}", align_bytes=256)
-                w_scales[g, m] = keep.tile([P, P], U8, name=f"w_scales{g}{m}", align_bytes=256)
+                w_grouped[g, m] = keep.tile([P, P, PACK], BF16, name=f"w_grouped{g}{m}", align_bytes=512)
+                w_codes[g, m] = keep.tile([P, P], U32, name=f"w_codes{g}{m}", align_bytes=512)
+                w_scales[g, m] = keep.tile([P, P], U8, name=f"w_scales{g}{m}", align_bytes=512)
         acc = [[psum.tile([P, HALF], F32, name=f"acc{m}{c}") for c in range(2)] for m in range(ROW_TILES)]
 
 
         def cast(copy, l):
-            narrow[l] = keep.tile([P, T], BF16, name=f"narrow{l}", align_bytes=256)
+            narrow[l] = keep.tile([P, T], BF16, name=f"narrow{l}", align_bytes=512)
             copy(out=narrow[l][:], in_=tables[l])
 
         def gather(l, v0, v1):
@@ -87,7 +87,7 @@ def tile_picked_grid_lin_none_sub_l_kernel(tc, xT, w, offs, out):
                 nc.vector.tensor_copy(dst, tables[l].indirect(entries))
 
         def weave(g, c, tag):
-            woven[g, c] = keep.tile([P, HALF * PACK], BF16, name=f"woven{g}{c}", tag=tag, align_bytes=256)
+            woven[g, c] = keep.tile([P, HALF * PACK], BF16, name=f"woven{g}{c}", tag=tag, align_bytes=512)
             words = pairs[g][:].bitcast(I32).rearrange("p (a v) -> p a v", a=2)
             nc.vector.tensor_copy(
                 out=woven[g, c][:].bitcast(I32).rearrange("p (v a) -> p v a", a=2),
@@ -95,8 +95,8 @@ def tile_picked_grid_lin_none_sub_l_kernel(tc, xT, w, offs, out):
             )
 
         def quantize_x(g, c, tag):
-            codes[g, c] = keep.tile([P, HALF], U32, name=f"codes{g}{c}", tag=tag, align_bytes=256)
-            scales[g, c] = keep.tile([P, HALF], U8, name=f"scales{g}{c}", align_bytes=256)
+            codes[g, c] = keep.tile([P, HALF], U32, name=f"codes{g}{c}", tag=tag, align_bytes=512)
+            scales[g, c] = keep.tile([P, HALF], U8, name=f"scales{g}{c}", align_bytes=512)
             nc.vector.quantize_mx(out=codes[g, c][:].bitcast(FP8X4), scales=scales[g, c][:], in_=woven[g, c][:])
 
         def interleave_w(copy, g, m, n0, n1):
@@ -124,7 +124,7 @@ def tile_picked_grid_lin_none_sub_l_kernel(tc, xT, w, offs, out):
             )
 
         def store(copy, queue, m, c, tag):
-            res = keep.tile([P, HALF], F32, name=f"res{m}{c}", tag=tag, align_bytes=256)
+            res = keep.tile([P, HALF], F32, name=f"res{m}{c}", tag=tag, align_bytes=512)
             copy(out=res[:], in_=acc[m][c][:])
             queue.dma_start(out=out[m * P : (m + 1) * P, c * HALF : (c + 1) * HALF], in_=res[:])
 

@@ -23,6 +23,7 @@ ROW_TILES = N // P
 HALF = V // 2
 LIST_ROWS = 16
 LINE = 4
+ALIGN = 512
 
 
 def tile_picked_grid_lin_none_sub_l_kernel(tc, xT, w, offs, out):
@@ -31,7 +32,7 @@ def tile_picked_grid_lin_none_sub_l_kernel(tc, xT, w, offs, out):
         keep = ctx.enter_context(tc.tile_pool(name="keep", bufs=1))
         psum = ctx.enter_context(tc.psum_pool(name="psum", bufs=1))
 
-        offsets = keep.tile([P, D * V // LIST_ROWS], U16, name="offsets", align_bytes=512)
+        offsets = keep.tile([P, D * V // LIST_ROWS], U16, name="offsets", align_bytes=ALIGN)
 
         warm = keep.tile([P, 1], F32, name="warm")
         warm_out = keep.tile([P, 1], F32, name="warm_out")
@@ -40,25 +41,29 @@ def tile_picked_grid_lin_none_sub_l_kernel(tc, xT, w, offs, out):
 
         on_scalar, on_vector = nc.scalar.copy, nc.vector.tensor_copy
 
-        first = keep.tile([P, 2 * T], F32, name="first", align_bytes=512)
-        nc.sync.dma_start(out=first[:], in_=xT[0:K_PASS, :].rearrange("(p j) t -> p (j t)", j=PACK)[:, 0 : 2 * T])
-        tables = {0: first[:, 0:T], 1: first[:, T : 2 * T]}
+        tables = {}
+
+        def load_tables(l0, count):
+            g, j = divmod(l0, PACK)
+            tile = keep.tile([P, count * T], F32, name=f"table{l0}", align_bytes=ALIGN)
+            rows = xT[g * K_PASS : (g + 1) * K_PASS, :].rearrange("(p j) t -> p (j t)", j=PACK)
+            nc.sync.dma_start(out=tile[:], in_=rows[:, j * T : (j + count) * T])
+            for i in range(count):
+                tables[l0 + i] = tile[:, i * T : (i + 1) * T]
+
+        load_tables(0, 2)
         nc.sync.dma_start(offsets[:], offs)
         for l in range(2, D):
-            g, j = divmod(l, PACK)
-            table = keep.tile([P, T], F32, name=f"table{l}", align_bytes=512)
-            rows = xT[g * K_PASS : (g + 1) * K_PASS, :].rearrange("(p j) t -> p j t", j=PACK)
-            nc.sync.dma_start(out=table[:], in_=rows[:, j, :])
-            tables[l] = table[:]
+            load_tables(l, 1)
         w_raw = {}
         for m in range(ROW_TILES):
             for g in range(PASSES):
-                w_raw[g, m] = keep.tile([P, PACK, P], F32, name=f"w_raw{g}{m}", align_bytes=512)
+                w_raw[g, m] = keep.tile([P, PACK, P], F32, name=f"w_raw{g}{m}", align_bytes=ALIGN)
                 rows = w[g * K_PASS : (g + 1) * K_PASS, m * P : (m + 1) * P].rearrange("(p j) n -> p j n", j=PACK)
                 nc.sync.dma_start(out=w_raw[g, m][:], in_=rows)
 
-        pairs = [keep.tile([P, PACK * V], BF16, name=f"pairs{g}", align_bytes=512) for g in range(PASSES)]
-        narrow = {}
+        planes = [keep.tile([P, 2 * V], F32, name=f"planes{g}", align_bytes=ALIGN) for g in range(PASSES)]
+        pairs = [keep.tile([P, PACK * V], BF16, name=f"pairs{g}", align_bytes=ALIGN) for g in range(PASSES)]
         woven = {}
         codes = {}
         scales = {}
@@ -67,36 +72,45 @@ def tile_picked_grid_lin_none_sub_l_kernel(tc, xT, w, offs, out):
         w_scales = {}
         for g in range(PASSES):
             for m in range(ROW_TILES):
-                w_grouped[g, m] = keep.tile([P, P, PACK], BF16, name=f"w_grouped{g}{m}", align_bytes=512)
-                w_codes[g, m] = keep.tile([P, P], U32, name=f"w_codes{g}{m}", align_bytes=512)
-                w_scales[g, m] = keep.tile([P, P], U8, name=f"w_scales{g}{m}", align_bytes=512)
+                w_grouped[g, m] = keep.tile([P, P, PACK], BF16, name=f"w_grouped{g}{m}", align_bytes=ALIGN)
+                w_codes[g, m] = keep.tile([P, P], U32, name=f"w_codes{g}{m}", align_bytes=ALIGN)
+                w_scales[g, m] = keep.tile([P, P], U8, name=f"w_scales{g}{m}", align_bytes=ALIGN)
         acc = [[psum.tile([P, HALF], F32, name=f"acc{m}{c}") for c in range(2)] for m in range(ROW_TILES)]
 
+        def pair_rows(g):
+            return pairs[g][:].rearrange("p (c a v e) -> p c a v e", c=2, a=2, e=2)
 
-        def cast(copy, l):
-            narrow[l] = keep.tile([P, T], BF16, name=f"narrow{l}", align_bytes=512)
-            copy(out=narrow[l][:], in_=tables[l])
+        def plane(g, c, e):
+            return planes[g][:, (2 * c + e) * HALF : (2 * c + e + 1) * HALF]
 
-        def gather(l, v0, v1):
+        def gather(l, c0, c1):
             g, j = divmod(l, PACK)
-            dst = pairs[g][:].rearrange("p (a v e) -> p a v e", a=2, e=2)[:, j // 2, v0:v1, j % 2]
-            entries = offsets[:, (l * V + v0) // LIST_ROWS : (l * V + v1) // LIST_ROWS]
+            entries = entries_of(l, c0 * HALF, c1 * HALF)
             if j < 2:
-                nc.scalar.activation(dst, narrow[l][:].indirect(entries), COPY)
+                nc.scalar.activation(plane(g, c0, j), tables[l].indirect(entries), COPY)
             else:
-                nc.vector.tensor_copy(dst, tables[l].indirect(entries))
+                nc.vector.tensor_copy(pair_rows(g)[:, c0:c1, 1, :, j % 2], tables[l].indirect(entries))
+
+        def pair(copy, g, c):
+            copy(
+                out=pair_rows(g)[:, c, 0, :, :],
+                in_=planes[g][:, c * V : (c + 1) * V].rearrange("p (e v) -> p v e", e=2),
+            )
+
+        def entries_of(l, v0, v1):
+            return offsets[:, (l * V + v0) // LIST_ROWS : (l * V + v1) // LIST_ROWS]
 
         def weave(g, c, tag):
-            woven[g, c] = keep.tile([P, HALF * PACK], BF16, name=f"woven{g}{c}", tag=tag, align_bytes=512)
-            words = pairs[g][:].bitcast(I32).rearrange("p (a v) -> p a v", a=2)
+            woven[g, c] = keep.tile([P, HALF * PACK], BF16, name=f"woven{g}{c}", tag=tag, align_bytes=ALIGN)
+            words = pairs[g][:].bitcast(I32)[:, c * V : (c + 1) * V]
             nc.vector.tensor_copy(
                 out=woven[g, c][:].bitcast(I32).rearrange("p (v a) -> p v a", a=2),
-                in_=words[:, :, c * HALF : (c + 1) * HALF].rearrange("p a v -> p v a"),
+                in_=words.rearrange("p (a v) -> p v a", a=2),
             )
 
         def quantize_x(g, c, tag):
-            codes[g, c] = keep.tile([P, HALF], U32, name=f"codes{g}{c}", tag=tag, align_bytes=512)
-            scales[g, c] = keep.tile([P, HALF], U8, name=f"scales{g}{c}", align_bytes=512)
+            codes[g, c] = keep.tile([P, HALF], U32, name=f"codes{g}{c}", tag=tag, align_bytes=ALIGN)
+            scales[g, c] = keep.tile([P, HALF], U8, name=f"scales{g}{c}", align_bytes=ALIGN)
             nc.vector.quantize_mx(out=codes[g, c][:].bitcast(FP8X4), scales=scales[g, c][:], in_=woven[g, c][:])
 
         def interleave_w(copy, g, m, n0, n1):
@@ -124,29 +138,33 @@ def tile_picked_grid_lin_none_sub_l_kernel(tc, xT, w, offs, out):
             )
 
         def store(copy, queue, m, c, tag):
-            res = keep.tile([P, HALF], F32, name=f"res{m}{c}", tag=tag, align_bytes=512)
+            res = keep.tile([P, HALF], F32, name=f"res{m}{c}", tag=tag, align_bytes=ALIGN)
             copy(out=res[:], in_=acc[m][c][:])
             queue.dma_start(out=out[m * P : (m + 1) * P, c * HALF : (c + 1) * HALF], in_=res[:])
 
-        cast(on_vector, 0)
-        gather(0, 0, V)
-        cast(on_vector, 1)
-        gather(1, 0, V)
-        gather(2, 0, V)
-        gather(3, 0, HALF)
-        gather(3, HALF, V)
+        nc.scalar.activation(planes[0][:, 0:V], tables[0].indirect(entries_of(0, 0, V)), COPY)
+        nc.vector.tensor_copy(planes[0][:, V : 2 * V], tables[1].indirect(entries_of(1, 0, V)))
+        on_scalar(
+            out=pair_rows(0)[:, :, 0, :, :],
+            in_=planes[0][:].rearrange("p (e c v) -> p c v e", e=2, c=2),
+        )
+        gather(2, 0, 2)
+        gather(3, 0, 1)
+        gather(3, 1, 2)
         weave(0, 0, "woven00")
         weave(0, 1, "woven01")
         quantize_x(0, 0, "codes00")
         quantize_x(0, 1, "codes01")
 
-        cast(on_scalar, 4)
-        gather(4, 0, V)
-        cast(on_vector, 5)
-        gather(5, 0, V)
-        gather(6, 0, V)
-        gather(7, 0, HALF)
-        gather(7, HALF, V)
+        gather(4, 0, 1)
+        gather(4, 1, 2)
+        nc.vector.tensor_copy(plane(1, 0, 1), tables[5].indirect(entries_of(5, 0, HALF)))
+        gather(5, 1, 2)
+        pair(on_scalar, 1, 1)
+        pair(on_scalar, 1, 0)
+        gather(6, 0, 2)
+        gather(7, 0, 1)
+        gather(7, 1, 2)
 
         weave(1, 0, "woven10")
         interleave_w(on_scalar, 0, 0, 0, P)

@@ -41,6 +41,9 @@ def tile_picked_grid_lin_none_sub_l_kernel(tc, xT, w, offs, out):
 
         on_scalar, on_vector = nc.scalar.copy, nc.vector.tensor_copy
 
+        def on_gpsimd(out, in_):
+            nc.gpsimd.tensor_scalar(out, in_, 1.0, 0.0, mybir.AluOpType.mult, mybir.AluOpType.add)
+
         tables = {}
 
         def load_tables(l0, count):
@@ -53,7 +56,9 @@ def tile_picked_grid_lin_none_sub_l_kernel(tc, xT, w, offs, out):
 
         load_tables(0, 2)
         nc.sync.dma_start(offsets[:], offs)
-        for l in range(2, D):
+        load_tables(2, 2)
+        load_tables(4, 2)
+        for l in range(6, D):
             load_tables(l, 1)
         w_raw = {}
         for m in range(ROW_TILES):
@@ -62,7 +67,7 @@ def tile_picked_grid_lin_none_sub_l_kernel(tc, xT, w, offs, out):
                 rows = w[g * K_PASS : (g + 1) * K_PASS, m * P : (m + 1) * P].rearrange("(p j) n -> p j n", j=PACK)
                 nc.sync.dma_start(out=w_raw[g, m][:], in_=rows)
 
-        planes = [keep.tile([P, 2 * V], F32, name=f"planes{g}", align_bytes=ALIGN) for g in range(PASSES)]
+        planes = [keep.tile([P, PACK * V], F32, name=f"planes{g}", align_bytes=ALIGN) for g in range(PASSES)]
         pairs = [keep.tile([P, PACK * V], BF16, name=f"pairs{g}", align_bytes=ALIGN) for g in range(PASSES)]
         woven = {}
         codes = {}
@@ -144,24 +149,27 @@ def tile_picked_grid_lin_none_sub_l_kernel(tc, xT, w, offs, out):
 
         nc.scalar.activation(planes[0][:, 0:V], tables[0].indirect(entries_of(0, 0, V)), COPY)
         nc.vector.tensor_copy(planes[0][:, V : 2 * V], tables[1].indirect(entries_of(1, 0, V)))
-        on_scalar(
-            out=pair_rows(0)[:, :, 0, :, :],
-            in_=planes[0][:].rearrange("p (e c v) -> p c v e", e=2, c=2),
-        )
-        gather(2, 0, 2)
+        by_level = planes[0][:].rearrange("p (j c v) -> p c j v", j=PACK, c=2)
+        on_vector(out=pair_rows(0)[:, 0, 0, :, :], in_=by_level[:, 0, 0:2, :].rearrange("p e v -> p v e"))
+        gather(2, 0, 1)
         gather(3, 0, 1)
-        gather(3, 1, 2)
+        for j in (2, 3):
+            nc.scalar.activation(by_level[:, 1, j, :], tables[j].indirect(entries_of(j, HALF, V)), COPY)
         weave(0, 0, "woven00")
-        weave(0, 1, "woven01")
+        woven[0, 1] = keep.tile([P, HALF * PACK], BF16, name="woven01", align_bytes=ALIGN)
+        on_vector(
+            out=woven[0, 1][:].rearrange("p (b i j) -> p b j i", i=LINE, j=PACK),
+            in_=by_level[:, 1, :, :].rearrange("p j (b i) -> p b j i", i=LINE),
+        )
         quantize_x(0, 0, "codes00")
         quantize_x(0, 1, "codes01")
 
         gather(4, 0, 1)
+        gather(5, 0, 1)
         gather(4, 1, 2)
-        nc.vector.tensor_copy(plane(1, 0, 1), tables[5].indirect(entries_of(5, 0, HALF)))
         gather(5, 1, 2)
-        pair(on_scalar, 1, 1)
-        pair(on_scalar, 1, 0)
+        pair(on_gpsimd, 1, 0)
+        pair(on_gpsimd, 1, 1)
         gather(6, 0, 2)
         gather(7, 0, 1)
         gather(7, 1, 2)

@@ -23,6 +23,7 @@ ROW_TILES = N // P
 HALF = V // 2
 LIST_ROWS = 16
 LINE = 4
+SHARE = 128
 ALIGN = 512
 
 
@@ -57,8 +58,7 @@ def tile_picked_grid_lin_none_sub_l_kernel(tc, xT, w, offs, out):
         load_tables(0, 2)
         nc.sync.dma_start(offsets[:], offs)
         load_tables(2, 2)
-        load_tables(4, 2)
-        for l in range(6, D):
+        for l in range(PACK, D):
             load_tables(l, 1)
         w_raw = {}
         for m in range(ROW_TILES):
@@ -68,6 +68,7 @@ def tile_picked_grid_lin_none_sub_l_kernel(tc, xT, w, offs, out):
                 nc.sync.dma_start(out=w_raw[g, m][:], in_=rows)
 
         planes = [keep.tile([P, PACK * V], F32, name=f"planes{g}", align_bytes=ALIGN) for g in range(PASSES)]
+        late = keep.tile([P, 2 * SHARE], F32, name="late", align_bytes=ALIGN)
         pairs = [keep.tile([P, PACK * V], BF16, name=f"pairs{g}", align_bytes=ALIGN) for g in range(PASSES)]
         woven = {}
         codes = {}
@@ -165,22 +166,26 @@ def tile_picked_grid_lin_none_sub_l_kernel(tc, xT, w, offs, out):
         quantize_x(0, 1, "codes01")
 
         gather(4, 0, 1)
-        gather(5, 0, 1)
         gather(4, 1, 2)
+        gather(5, 0, 1)
         gather(5, 1, 2)
         pair(on_gpsimd, 1, 0)
         pair(on_gpsimd, 1, 1)
-        gather(6, 0, 2)
-        gather(7, 0, 1)
-        gather(7, 1, 2)
+        own = HALF - SHARE
+        for e in range(2):
+            l = 6 + e
+            gather(l, 0, 1)
+            nc.vector.tensor_copy(pair_rows(1)[:, 1, 1, 0:own, e], tables[l].indirect(entries_of(l, HALF, HALF + own)))
+            nc.scalar.activation(late[:, e * SHARE : (e + 1) * SHARE], tables[l].indirect(entries_of(l, HALF + own, V)), COPY)
 
+        on_gpsimd(out=pair_rows(1)[:, 1, 1, own:HALF, :], in_=late[:].rearrange("p (e v) -> p v e", e=2))
         weave(1, 0, "woven10")
+        weave(1, 1, "woven11")
         interleave_w(on_scalar, 0, 0, 0, P)
         quantize_w(0, 0)
         multiply(0, 0, 0, True)
         multiply(0, 0, 1, True)
-        weave(1, 1, "w_raw00")
-        quantize_x(1, 0, "w_grouped00")
+        quantize_x(1, 0, "w_raw00")
         interleave_w(on_scalar, 1, 0, 0, P)
         quantize_w(1, 0)
         multiply(1, 0, 0, False)
@@ -190,13 +195,13 @@ def tile_picked_grid_lin_none_sub_l_kernel(tc, xT, w, offs, out):
         interleave_w(on_scalar, 0, 1, 0, P)
         quantize_w(0, 1)
         multiply(0, 1, 0, True)
+        multiply(0, 1, 1, True)
         interleave_w(on_scalar, 1, 1, 0, P)
         quantize_w(1, 1)
         multiply(1, 1, 0, False)
-        multiply(1, 1, 1, True)
-        multiply(0, 1, 1, False)
+        multiply(1, 1, 1, False)
 
-        store(on_scalar, nc.scalar, 0, 0, "w_raw11")
-        store(on_vector, nc.sync, 0, 1, "w_grouped11")
-        store(on_scalar, nc.scalar, 1, 0, "res10")
+        store(on_scalar, nc.sync, 0, 0, "w_grouped01")
+        store(on_scalar, nc.sync, 0, 1, "res01")
+        store(on_scalar, nc.sync, 1, 0, "res10")
         store(on_vector, nc.sync, 1, 1, "res11")

@@ -24,6 +24,7 @@ HALF = V // 2
 LIST_ROWS = 16
 LINE = 4
 SHARE = 128
+W_SHARE = 32
 ALIGN = 512
 
 
@@ -61,8 +62,8 @@ def tile_picked_grid_lin_none_sub_l_kernel(tc, xT, w, offs, out):
         for l in range(PACK, D):
             load_tables(l, 1)
         w_raw = {}
-        for m in range(ROW_TILES):
-            for g in range(PASSES):
+        for g in range(PASSES):
+            for m in range(ROW_TILES):
                 w_raw[g, m] = keep.tile([P, PACK, P], F32, name=f"w_raw{g}{m}", align_bytes=ALIGN)
                 rows = w[g * K_PASS : (g + 1) * K_PASS, m * P : (m + 1) * P].rearrange("(p j) n -> p j n", j=PACK)
                 nc.sync.dma_start(out=w_raw[g, m][:], in_=rows)
@@ -180,28 +181,28 @@ def tile_picked_grid_lin_none_sub_l_kernel(tc, xT, w, offs, out):
 
         on_gpsimd(out=pair_rows(1)[:, 1, 1, own:HALF, :], in_=late[:].rearrange("p (e v) -> p v e", e=2))
         weave(1, 0, "woven10")
-        weave(1, 1, "woven11")
         interleave_w(on_scalar, 0, 0, 0, P)
+        interleave_w(on_vector, 0, 1, P - W_SHARE, P)
         quantize_w(0, 0)
         multiply(0, 0, 0, True)
         multiply(0, 0, 1, True)
-        quantize_x(1, 0, "w_raw00")
+        weave(1, 1, "w_raw00")
+        interleave_w(on_scalar, 0, 1, 0, P - W_SHARE)
+        quantize_w(0, 1)
+        multiply(0, 1, 0, True)
+        multiply(0, 1, 1, True)
+        quantize_x(1, 0, "w_raw01")
         interleave_w(on_scalar, 1, 0, 0, P)
         quantize_w(1, 0)
         multiply(1, 0, 0, False)
         quantize_x(1, 1, "w_raw10")
         multiply(1, 0, 1, False)
-
-        interleave_w(on_scalar, 0, 1, 0, P)
-        quantize_w(0, 1)
-        multiply(0, 1, 0, True)
-        multiply(0, 1, 1, True)
         interleave_w(on_scalar, 1, 1, 0, P)
         quantize_w(1, 1)
         multiply(1, 1, 0, False)
         multiply(1, 1, 1, False)
 
-        store(on_scalar, nc.sync, 0, 0, "w_grouped01")
-        store(on_scalar, nc.sync, 0, 1, "res01")
+        store(on_scalar, nc.sync, 0, 0, "res00")
+        store(on_vector, nc.sync, 0, 1, "w_grouped10")
         store(on_scalar, nc.sync, 1, 0, "res10")
         store(on_vector, nc.sync, 1, 1, "res11")

@@ -25,6 +25,7 @@ LIST_ROWS = 16
 LINE = 4
 SHARE = 128
 W_SHARE = 32
+BANK = 128
 ALIGN = 512
 
 
@@ -82,7 +83,10 @@ def tile_picked_grid_lin_none_sub_l_kernel(tc, xT, w, offs, out):
                 w_grouped[g, m] = keep.tile([P, P, PACK], BF16, name=f"w_grouped{g}{m}", align_bytes=ALIGN)
                 w_codes[g, m] = keep.tile([P, P], U32, name=f"w_codes{g}{m}", align_bytes=ALIGN)
                 w_scales[g, m] = keep.tile([P, P], U8, name=f"w_scales{g}{m}", align_bytes=ALIGN)
-        acc = [[psum.tile([P, HALF], F32, name=f"acc{m}{c}") for c in range(2)] for m in range(ROW_TILES)]
+        acc = {}
+        for m in range(ROW_TILES):
+            for q in range(V // BANK):
+                acc[m, q] = psum.tile([P, BANK], F32, name=f"acc{m}{q}")
 
         def pair_rows(g):
             return pairs[g][:].rearrange("p (c a v e) -> p c a v e", c=2, a=2, e=2)
@@ -134,19 +138,21 @@ def tile_picked_grid_lin_none_sub_l_kernel(tc, xT, w, offs, out):
             )
 
         def multiply(g, m, c, opens):
-            nc.tensor.matmul_mx(
-                out=acc[m][c][:],
-                lhsT=w_codes[g, m][:].bitcast(FP8X4),
-                lhsT_scale=w_scales[g, m][:],
-                rhs=codes[g, c][:].bitcast(FP8X4),
-                rhs_scale=scales[g, c][:],
-                start=opens,
-                stop=not opens,
-            )
+            for h in range(HALF // BANK):
+                nc.tensor.matmul_mx(
+                    out=acc[m, 2 * c + h][:],
+                    lhsT=w_codes[g, m][:].bitcast(FP8X4),
+                    lhsT_scale=w_scales[g, m][:],
+                    rhs=codes[g, c][:, h * BANK : (h + 1) * BANK].bitcast(FP8X4),
+                    rhs_scale=scales[g, c][:, h * BANK : (h + 1) * BANK],
+                    start=opens,
+                    stop=not opens,
+                )
 
         def store(copy, queue, m, c, tag):
             res = keep.tile([P, HALF], F32, name=f"res{m}{c}", tag=tag, align_bytes=ALIGN)
-            copy(out=res[:], in_=acc[m][c][:])
+            for h in range(HALF // BANK):
+                copy(out=res[:, h * BANK : (h + 1) * BANK], in_=acc[m, 2 * c + h][:])
             queue.dma_start(out=out[m * P : (m + 1) * P, c * HALF : (c + 1) * HALF], in_=res[:])
 
         nc.scalar.activation(planes[0][:, 0:V], tables[0].indirect(entries_of(0, 0, V)), COPY)

@@ -21,11 +21,12 @@ K_PASS = P * PACK
 PASSES = K // K_PASS
 ROW_TILES = N // P
 HALF = V // 2
+BANK = 128
 LIST_ROWS = 16
 LINE = 4
 SHARE = 128
 W_SHARE = 32
-BANK = 128
+STAGGER = 64
 ALIGN = 512
 
 
@@ -42,9 +43,9 @@ def tile_picked_grid_lin_none_sub_l_kernel(tc, xT, w, offs, out):
         nc.vector.memset(warm[:], 0.0)
         nc.scalar.activation(warm_out[:], warm[:], COPY)
 
-        on_scalar, on_vector = nc.scalar.copy, nc.vector.tensor_copy
+        copy_on_scalar, copy_on_vector = nc.scalar.copy, nc.vector.tensor_copy
 
-        def on_gpsimd(out, in_):
+        def copy_on_gpsimd(out, in_):
             nc.gpsimd.tensor_scalar(out, in_, 1.0, 0.0, mybir.AluOpType.mult, mybir.AluOpType.add)
 
         tables = {}
@@ -70,7 +71,7 @@ def tile_picked_grid_lin_none_sub_l_kernel(tc, xT, w, offs, out):
                 nc.sync.dma_start(out=w_raw[g, m][:], in_=rows)
 
         planes = [keep.tile([P, PACK * V], F32, name=f"planes{g}", align_bytes=ALIGN) for g in range(PASSES)]
-        late = keep.tile([P, 2 * SHARE], F32, name="late", align_bytes=ALIGN)
+        share_planes = keep.tile([P, 2 * SHARE], F32, name="share_planes", align_bytes=ALIGN)
         pairs = [keep.tile([P, PACK * V], BF16, name=f"pairs{g}", align_bytes=ALIGN) for g in range(PASSES)]
         woven = {}
         codes = {}
@@ -81,134 +82,131 @@ def tile_picked_grid_lin_none_sub_l_kernel(tc, xT, w, offs, out):
         for g in range(PASSES):
             for m in range(ROW_TILES):
                 w_grouped[g, m] = keep.tile([P, P, PACK], BF16, name=f"w_grouped{g}{m}", align_bytes=ALIGN)
-                w_codes[g, m] = keep.tile([P, P], U32, name=f"w_codes{g}{m}", align_bytes=ALIGN)
-                w_scales[g, m] = keep.tile([P, P], U8, name=f"w_scales{g}{m}", align_bytes=ALIGN)
+                words = keep.tile([P, STAGGER // 2 + P], U32, name=f"w_codes{g}{m}", align_bytes=ALIGN)
+                w_codes[g, m] = words[:, STAGGER // 2 :]
+                plane = keep.tile([P, 3 * STAGGER + P], U8, name=f"w_scales{g}{m}", align_bytes=ALIGN)
+                w_scales[g, m] = plane[:, 3 * STAGGER :]
         acc = {}
         for m in range(ROW_TILES):
             for q in range(V // BANK):
                 acc[m, q] = psum.tile([P, BANK], F32, name=f"acc{m}{q}")
 
-        def pair_rows(g):
-            return pairs[g][:].rearrange("p (c a v e) -> p c a v e", c=2, a=2, e=2)
 
-        def plane(g, c, e):
-            return planes[g][:, (2 * c + e) * HALF : (2 * c + e + 1) * HALF]
+        def looked_up(l, v0, v1):
+            return tables[l].indirect(offsets[:, (l * V + v0) // LIST_ROWS : (l * V + v1) // LIST_ROWS])
 
-        def gather(l, c0, c1):
+        def gather_on_scalar(plane, l, v0, v1):
+            nc.scalar.activation(plane, looked_up(l, v0, v1), COPY)
+
+        def pair_row(g, c, a):
+            return pairs[g][:].rearrange("p (c a v e) -> p c a v e", c=2, a=2, e=2)[:, c, a, :, :]
+
+        def gather_into_pair_row(l, v0, v1):
             g, j = divmod(l, PACK)
-            entries = entries_of(l, c0 * HALF, c1 * HALF)
-            if j < 2:
-                nc.scalar.activation(plane(g, c0, j), tables[l].indirect(entries), COPY)
-            else:
-                nc.vector.tensor_copy(pair_rows(g)[:, c0:c1, 1, :, j % 2], tables[l].indirect(entries))
+            c = v0 // HALF
+            nc.vector.tensor_copy(pair_row(g, c, j // 2)[:, v0 - c * HALF : v1 - c * HALF, j % 2], looked_up(l, v0, v1))
 
-        def pair(copy, g, c):
-            copy(
-                out=pair_rows(g)[:, c, 0, :, :],
-                in_=planes[g][:, c * V : (c + 1) * V].rearrange("p (e v) -> p v e", e=2),
-            )
-
-        def entries_of(l, v0, v1):
-            return offsets[:, (l * V + v0) // LIST_ROWS : (l * V + v1) // LIST_ROWS]
+        def pair(copy, row, two_planes):
+            copy(out=row, in_=two_planes.rearrange("p e v -> p v e"))
 
         def weave(g, c, tag):
             woven[g, c] = keep.tile([P, HALF * PACK], BF16, name=f"woven{g}{c}", tag=tag, align_bytes=ALIGN)
-            words = pairs[g][:].bitcast(I32)[:, c * V : (c + 1) * V]
+            both_rows = pairs[g][:].bitcast(I32)[:, 2 * c * HALF : 2 * (c + 1) * HALF]
             nc.vector.tensor_copy(
                 out=woven[g, c][:].bitcast(I32).rearrange("p (v a) -> p v a", a=2),
-                in_=words.rearrange("p (a v) -> p v a", a=2),
+                in_=both_rows.rearrange("p (a v) -> p v a", a=2),
             )
+
+        def interleave(copy, grouped, four_rows):
+            copy(
+                out=grouped.rearrange("p (b i) j -> p b j i", i=LINE),
+                in_=four_rows.rearrange("p j (b i) -> p b j i", i=LINE),
+            )
+
+        def interleave_w(copy, g, m, n0, n1):
+            interleave(copy, w_grouped[g, m][:, n0:n1, :], w_raw[g, m][:, :, n0:n1])
 
         def quantize_x(g, c, tag):
             codes[g, c] = keep.tile([P, HALF], U32, name=f"codes{g}{c}", tag=tag, align_bytes=ALIGN)
-            scales[g, c] = keep.tile([P, HALF], U8, name=f"scales{g}{c}", align_bytes=ALIGN)
-            nc.vector.quantize_mx(out=codes[g, c][:].bitcast(FP8X4), scales=scales[g, c][:], in_=woven[g, c][:])
-
-        def interleave_w(copy, g, m, n0, n1):
-            copy(
-                out=w_grouped[g, m][:, n0:n1, :].rearrange("p (b i) j -> p b j i", i=LINE),
-                in_=w_raw[g, m][:, :, n0:n1].rearrange("p j (b i) -> p b j i", i=LINE),
-            )
+            plane = keep.tile([P, STAGGER + HALF], U8, name=f"scales{g}{c}", align_bytes=ALIGN)
+            scales[g, c] = plane[:, STAGGER:]
+            nc.vector.quantize_mx(out=codes[g, c][:].bitcast(FP8X4), scales=scales[g, c], in_=woven[g, c][:])
 
         def quantize_w(g, m):
             nc.vector.quantize_mx(
-                out=w_codes[g, m][:].bitcast(FP8X4),
-                scales=w_scales[g, m][:],
+                out=w_codes[g, m].bitcast(FP8X4),
+                scales=w_scales[g, m],
                 in_=w_grouped[g, m][:].rearrange("p n j -> p (n j)"),
             )
 
-        def multiply(g, m, c, opens):
+        def multiply(g, m, c):
             for h in range(HALF // BANK):
                 nc.tensor.matmul_mx(
-                    out=acc[m, 2 * c + h][:],
-                    lhsT=w_codes[g, m][:].bitcast(FP8X4),
-                    lhsT_scale=w_scales[g, m][:],
+                    out=acc[m, c * HALF // BANK + h][:],
+                    lhsT=w_codes[g, m].bitcast(FP8X4),
+                    lhsT_scale=w_scales[g, m],
                     rhs=codes[g, c][:, h * BANK : (h + 1) * BANK].bitcast(FP8X4),
                     rhs_scale=scales[g, c][:, h * BANK : (h + 1) * BANK],
-                    start=opens,
-                    stop=not opens,
+                    start=g == 0,
+                    stop=g == PASSES - 1,
                 )
 
-        def store(copy, queue, m, c, tag):
+        def store(copy, m, c, tag):
             res = keep.tile([P, HALF], F32, name=f"res{m}{c}", tag=tag, align_bytes=ALIGN)
             for h in range(HALF // BANK):
-                copy(out=res[:, h * BANK : (h + 1) * BANK], in_=acc[m, 2 * c + h][:])
-            queue.dma_start(out=out[m * P : (m + 1) * P, c * HALF : (c + 1) * HALF], in_=res[:])
+                copy(out=res[:, h * BANK : (h + 1) * BANK], in_=acc[m, c * HALF // BANK + h][:])
+            nc.sync.dma_start(out=out[m * P : (m + 1) * P, c * HALF : (c + 1) * HALF], in_=res[:])
 
-        nc.scalar.activation(planes[0][:, 0:V], tables[0].indirect(entries_of(0, 0, V)), COPY)
-        nc.vector.tensor_copy(planes[0][:, V : 2 * V], tables[1].indirect(entries_of(1, 0, V)))
-        by_level = planes[0][:].rearrange("p (j c v) -> p c j v", j=PACK, c=2)
-        on_vector(out=pair_rows(0)[:, 0, 0, :, :], in_=by_level[:, 0, 0:2, :].rearrange("p e v -> p v e"))
-        gather(2, 0, 1)
-        gather(3, 0, 1)
-        for j in (2, 3):
-            nc.scalar.activation(by_level[:, 1, j, :], tables[j].indirect(entries_of(j, HALF, V)), COPY)
+        gather_on_scalar(planes[0][:, 0:V], 0, 0, V)
+        nc.vector.tensor_copy(planes[0][:, V : 2 * V], looked_up(1, 0, V))
+        planes_of_half = planes[0][:].rearrange("p (j c v) -> p c j v", j=PACK, c=2)
+        pair(copy_on_vector, pair_row(0, 0, 0), planes_of_half[:, 0, 0:2, :])
+        for l in (2, 3):
+            gather_into_pair_row(l, 0, HALF)
+        for l in (2, 3):
+            gather_on_scalar(planes_of_half[:, 1, l, :], l, HALF, V)
         weave(0, 0, "woven00")
         woven[0, 1] = keep.tile([P, HALF * PACK], BF16, name="woven01", align_bytes=ALIGN)
-        on_vector(
-            out=woven[0, 1][:].rearrange("p (b i j) -> p b j i", i=LINE, j=PACK),
-            in_=by_level[:, 1, :, :].rearrange("p j (b i) -> p b j i", i=LINE),
-        )
+        interleave(copy_on_vector, woven[0, 1][:].rearrange("p (v j) -> p v j", j=PACK), planes_of_half[:, 1, :, :])
         quantize_x(0, 0, "codes00")
         quantize_x(0, 1, "codes01")
 
-        gather(4, 0, 1)
-        gather(4, 1, 2)
-        gather(5, 0, 1)
-        gather(5, 1, 2)
-        pair(on_gpsimd, 1, 0)
-        pair(on_gpsimd, 1, 1)
-        own = HALF - SHARE
+        two_planes = planes[1][:, 0 : 2 * V].rearrange("p (c e v) -> p c e v", c=2, e=2)
         for e in range(2):
-            l = 6 + e
-            gather(l, 0, 1)
-            nc.vector.tensor_copy(pair_rows(1)[:, 1, 1, 0:own, e], tables[l].indirect(entries_of(l, HALF, HALF + own)))
-            nc.scalar.activation(late[:, e * SHARE : (e + 1) * SHARE], tables[l].indirect(entries_of(l, HALF + own, V)), COPY)
+            for c in range(2):
+                gather_on_scalar(two_planes[:, c, e, :], 4 + e, c * HALF, (c + 1) * HALF)
+        for c in range(2):
+            pair(copy_on_gpsimd, pair_row(1, c, 0), two_planes[:, c, :, :])
+        for e in range(2):
+            gather_into_pair_row(6 + e, 0, HALF)
+            gather_into_pair_row(6 + e, HALF, V - SHARE)
+            gather_on_scalar(share_planes[:, e * SHARE : (e + 1) * SHARE], 6 + e, V - SHARE, V)
+        pair(copy_on_gpsimd, pair_row(1, 1, 1)[:, HALF - SHARE : HALF, :], share_planes[:].rearrange("p (e v) -> p e v", e=2))
 
-        on_gpsimd(out=pair_rows(1)[:, 1, 1, own:HALF, :], in_=late[:].rearrange("p (e v) -> p v e", e=2))
         weave(1, 0, "woven10")
-        interleave_w(on_scalar, 0, 0, 0, P)
-        interleave_w(on_vector, 0, 1, P - W_SHARE, P)
+        interleave_w(copy_on_scalar, 0, 0, 0, P)
+        interleave_w(copy_on_vector, 0, 1, P - W_SHARE, P)
         quantize_w(0, 0)
-        multiply(0, 0, 0, True)
-        multiply(0, 0, 1, True)
+        multiply(0, 0, 0)
+        multiply(0, 0, 1)
         weave(1, 1, "w_raw00")
-        interleave_w(on_scalar, 0, 1, 0, P - W_SHARE)
+        interleave_w(copy_on_scalar, 0, 1, 0, P - W_SHARE)
         quantize_w(0, 1)
-        multiply(0, 1, 0, True)
-        multiply(0, 1, 1, True)
-        quantize_x(1, 0, "w_raw01")
-        interleave_w(on_scalar, 1, 0, 0, P)
-        quantize_w(1, 0)
-        multiply(1, 0, 0, False)
-        quantize_x(1, 1, "w_raw10")
-        multiply(1, 0, 1, False)
-        interleave_w(on_scalar, 1, 1, 0, P)
-        quantize_w(1, 1)
-        multiply(1, 1, 0, False)
-        multiply(1, 1, 1, False)
+        multiply(0, 1, 0)
+        multiply(0, 1, 1)
 
-        store(on_scalar, nc.sync, 0, 0, "res00")
-        store(on_vector, nc.sync, 0, 1, "w_grouped10")
-        store(on_scalar, nc.sync, 1, 0, "res10")
-        store(on_vector, nc.sync, 1, 1, "res11")
+        quantize_x(1, 0, "w_raw01")
+        interleave_w(copy_on_scalar, 1, 0, 0, P)
+        quantize_w(1, 0)
+        multiply(1, 0, 0)
+        quantize_x(1, 1, "w_raw10")
+        multiply(1, 0, 1)
+        interleave_w(copy_on_scalar, 1, 1, 0, P)
+        quantize_w(1, 1)
+        multiply(1, 1, 0)
+        multiply(1, 1, 1)
+
+        store(copy_on_scalar, 0, 0, "res00")
+        store(copy_on_vector, 0, 1, "w_grouped10")
+        store(copy_on_scalar, 1, 0, "res10")
+        store(copy_on_vector, 1, 1, "res11")

from contextlib import ExitStack

import concourse.mybir as mybir

K, T, D, V, N = 1024, 1024, 8, 512, 256
FLOPS = 2 * K * N * V

F32 = mybir.dt.float32
BF16 = mybir.dt.bfloat16
I32 = mybir.dt.int32
U32 = mybir.dt.uint32
U16 = mybir.dt.uint16
U8 = mybir.dt.uint8
FP8X4 = mybir.dt.float8_e4m3fn_x4

COPY = mybir.ActivationFunctionType.Copy

P = 128
PACK = 4
K_PASS = P * PACK
PASSES = K // K_PASS
ROW_TILES = N // P
HALF = V // 2
BANK = 128
LIST_ROWS = 16
LINE = 4
SHARE = 128
W_SHARE = 32
STAGGER = 64
ALIGN = 512


def tile_picked_grid_lin_none_sub_l_kernel(tc, xT, w, offs, out):
    nc = tc.nc
    with ExitStack() as ctx:
        keep = ctx.enter_context(tc.tile_pool(name="keep", bufs=1))
        psum = ctx.enter_context(tc.psum_pool(name="psum", bufs=1))

        offsets = keep.tile([P, D * V // LIST_ROWS], U16, name="offsets", align_bytes=ALIGN)

        warm = keep.tile([P, 1], F32, name="warm")
        warm_out = keep.tile([P, 1], F32, name="warm_out")
        nc.vector.memset(warm[:], 0.0)
        nc.scalar.activation(warm_out[:], warm[:], COPY)

        copy_on_scalar, copy_on_vector = nc.scalar.copy, nc.vector.tensor_copy

        def copy_on_gpsimd(out, in_):
            nc.gpsimd.tensor_scalar(out, in_, 1.0, 0.0, mybir.AluOpType.mult, mybir.AluOpType.add)

        tables = {}

        def load_tables(l0, count):
            g, j = divmod(l0, PACK)
            tile = keep.tile([P, count * T], F32, name=f"table{l0}", align_bytes=ALIGN)
            rows = xT[g * K_PASS : (g + 1) * K_PASS, :].rearrange("(p j) t -> p (j t)", j=PACK)
            nc.sync.dma_start(out=tile[:], in_=rows[:, j * T : (j + count) * T])
            for i in range(count):
                tables[l0 + i] = tile[:, i * T : (i + 1) * T]

        load_tables(0, 2)
        nc.sync.dma_start(offsets[:], offs)
        load_tables(2, 2)
        for l in range(PACK, D):
            load_tables(l, 1)
        w_raw = {}
        for g in range(PASSES):
            for m in range(ROW_TILES):
                w_raw[g, m] = keep.tile([P, PACK, P], F32, name=f"w_raw{g}{m}", align_bytes=ALIGN)
                rows = w[g * K_PASS : (g + 1) * K_PASS, m * P : (m + 1) * P].rearrange("(p j) n -> p j n", j=PACK)
                nc.sync.dma_start(out=w_raw[g, m][:], in_=rows)

        planes = [keep.tile([P, PACK * V], F32, name=f"planes{g}", align_bytes=ALIGN) for g in range(PASSES)]
        share_planes = keep.tile([P, 2 * SHARE], F32, name="share_planes", align_bytes=ALIGN)
        pairs = [keep.tile([P, PACK * V], BF16, name=f"pairs{g}", align_bytes=ALIGN) for g in range(PASSES)]
        woven = {}
        codes = {}
        scales = {}
        w_grouped = {}
        w_codes = {}
        w_scales = {}
        for g in range(PASSES):
            for m in range(ROW_TILES):
                w_grouped[g, m] = keep.tile([P, P, PACK], BF16, name=f"w_grouped{g}{m}", align_bytes=ALIGN)
                words = keep.tile([P, STAGGER // 2 + P], U32, name=f"w_codes{g}{m}", align_bytes=ALIGN)
                w_codes[g, m] = words[:, STAGGER // 2 :]
                plane = keep.tile([P, 3 * STAGGER + P], U8, name=f"w_scales{g}{m}", align_bytes=ALIGN)
                w_scales[g, m] = plane[:, 3 * STAGGER :]
        acc = {}
        for m in range(ROW_TILES):
            for q in range(V // BANK):
                acc[m, q] = psum.tile([P, BANK], F32, name=f"acc{m}{q}")


        def looked_up(l, v0, v1):
            return tables[l].indirect(offsets[:, (l * V + v0) // LIST_ROWS : (l * V + v1) // LIST_ROWS])

        def gather_on_scalar(plane, l, v0, v1):
            nc.scalar.activation(plane, looked_up(l, v0, v1), COPY)

        def pair_row(g, c, a):
            return pairs[g][:].rearrange("p (c a v e) -> p c a v e", c=2, a=2, e=2)[:, c, a, :, :]

        def gather_into_pair_row(l, v0, v1):
            g, j = divmod(l, PACK)
            c = v0 // HALF
            nc.vector.tensor_copy(pair_row(g, c, j // 2)[:, v0 - c * HALF : v1 - c * HALF, j % 2], looked_up(l, v0, v1))

        def pair(copy, row, two_planes):
            copy(out=row, in_=two_planes.rearrange("p e v -> p v e"))

        def weave(g, c, tag):
            woven[g, c] = keep.tile([P, HALF * PACK], BF16, name=f"woven{g}{c}", tag=tag, align_bytes=ALIGN)
            both_rows = pairs[g][:].bitcast(I32)[:, 2 * c * HALF : 2 * (c + 1) * HALF]
            nc.vector.tensor_copy(
                out=woven[g, c][:].bitcast(I32).rearrange("p (v a) -> p v a", a=2),
                in_=both_rows.rearrange("p (a v) -> p v a", a=2),
            )

        def interleave(copy, grouped, four_rows):
            copy(
                out=grouped.rearrange("p (b i) j -> p b j i", i=LINE),
                in_=four_rows.rearrange("p j (b i) -> p b j i", i=LINE),
            )

        def interleave_w(copy, g, m, n0, n1):
            interleave(copy, w_grouped[g, m][:, n0:n1, :], w_raw[g, m][:, :, n0:n1])

        def quantize_x(g, c, tag):
            codes[g, c] = keep.tile([P, HALF], U32, name=f"codes{g}{c}", tag=tag, align_bytes=ALIGN)
            plane = keep.tile([P, STAGGER + HALF], U8, name=f"scales{g}{c}", align_bytes=ALIGN)
            scales[g, c] = plane[:, STAGGER:]
            nc.vector.quantize_mx(out=codes[g, c][:].bitcast(FP8X4), scales=scales[g, c], in_=woven[g, c][:])

        def quantize_w(g, m):
            nc.vector.quantize_mx(
                out=w_codes[g, m].bitcast(FP8X4),
                scales=w_scales[g, m],
                in_=w_grouped[g, m][:].rearrange("p n j -> p (n j)"),
            )

        def multiply(g, m, c):
            for h in range(HALF // BANK):
                nc.tensor.matmul_mx(
                    out=acc[m, c * HALF // BANK + h][:],
                    lhsT=w_codes[g, m].bitcast(FP8X4),
                    lhsT_scale=w_scales[g, m],
                    rhs=codes[g, c][:, h * BANK : (h + 1) * BANK].bitcast(FP8X4),
                    rhs_scale=scales[g, c][:, h * BANK : (h + 1) * BANK],
                    start=g == 0,
                    stop=g == PASSES - 1,
                )

        def store(copy, m, c, tag):
            res = keep.tile([P, HALF], F32, name=f"res{m}{c}", tag=tag, align_bytes=ALIGN)
            for h in range(HALF // BANK):
                copy(out=res[:, h * BANK : (h + 1) * BANK], in_=acc[m, c * HALF // BANK + h][:])
            nc.sync.dma_start(out=out[m * P : (m + 1) * P, c * HALF : (c + 1) * HALF], in_=res[:])

        gather_on_scalar(planes[0][:, 0:V], 0, 0, V)
        nc.vector.tensor_copy(planes[0][:, V : 2 * V], looked_up(1, 0, V))
        planes_of_half = planes[0][:].rearrange("p (j c v) -> p c j v", j=PACK, c=2)
        pair(copy_on_vector, pair_row(0, 0, 0), planes_of_half[:, 0, 0:2, :])
        for l in (2, 3):
            gather_into_pair_row(l, 0, HALF)
        for l in (2, 3):
            gather_on_scalar(planes_of_half[:, 1, l, :], l, HALF, V)
        weave(0, 0, "woven00")
        woven[0, 1] = keep.tile([P, HALF * PACK], BF16, name="woven01", align_bytes=ALIGN)
        interleave(copy_on_vector, woven[0, 1][:].rearrange("p (v j) -> p v j", j=PACK), planes_of_half[:, 1, :, :])
        quantize_x(0, 0, "codes00")
        quantize_x(0, 1, "codes01")

        two_planes = planes[1][:, 0 : 2 * V].rearrange("p (c e v) -> p c e v", c=2, e=2)
        for e in range(2):
            for c in range(2):
                gather_on_scalar(two_planes[:, c, e, :], 4 + e, c * HALF, (c + 1) * HALF)
        for c in range(2):
            pair(copy_on_gpsimd, pair_row(1, c, 0), two_planes[:, c, :, :])
        for e in range(2):
            gather_into_pair_row(6 + e, 0, HALF)
            gather_into_pair_row(6 + e, HALF, V - SHARE)
            gather_on_scalar(share_planes[:, e * SHARE : (e + 1) * SHARE], 6 + e, V - SHARE, V)
        pair(copy_on_gpsimd, pair_row(1, 1, 1)[:, HALF - SHARE : HALF, :], share_planes[:].rearrange("p (e v) -> p e v", e=2))

        weave(1, 0, "woven10")
        interleave_w(copy_on_scalar, 0, 0, 0, P)
        interleave_w(copy_on_vector, 0, 1, P - W_SHARE, P)
        quantize_w(0, 0)
        multiply(0, 0, 0)
        multiply(0, 0, 1)
        weave(1, 1, "w_raw00")
        interleave_w(copy_on_scalar, 0, 1, 0, P - W_SHARE)
        quantize_w(0, 1)
        multiply(0, 1, 0)
        multiply(0, 1, 1)

        quantize_x(1, 0, "w_raw01")
        interleave_w(copy_on_scalar, 1, 0, 0, P)
        quantize_w(1, 0)
        multiply(1, 0, 0)
        quantize_x(1, 1, "w_raw10")
        multiply(1, 0, 1)
        interleave_w(copy_on_scalar, 1, 1, 0, P)
        quantize_w(1, 1)
        multiply(1, 1, 0)
        multiply(1, 1, 1)

        store(copy_on_scalar, 0, 0, "res00")
        store(copy_on_vector, 0, 1, "w_grouped10")
        store(copy_on_scalar, 1, 0, "res10")
        store(copy_on_vector, 1, 1, "res11")
